import numpy as np
import ml_dtypes


def mxq(x, axis, fmt="e4m3"):
    dtype, down = {"e4m3": (ml_dtypes.float8_e4m3fn, 7), "e5m2": (ml_dtypes.float8_e5m2, 14)}[fmt]
    v = np.moveaxis(np.asarray(x, np.float32).astype(ml_dtypes.bfloat16).astype(np.float64), axis, -1)
    blocks = v.reshape(v.shape[:-1] + (-1, 32))
    amax = np.abs(blocks).max(-1, keepdims=True)
    byte = np.maximum(np.where(amax > 0, np.frexp(amax)[1] - 1 + 127, 0) - down, 1)
    scale = np.exp2(byte - 127.0)
    codes = (blocks / scale).astype(np.float32).astype(dtype).astype(np.float64)
    return np.moveaxis((codes * scale).reshape(v.shape), -1, axis)


WIDE = False


def mx_kscale(k):
    if not WIDE:
        return np.ones(k)
    levels = np.array([10, -10, 5, -5, 0])
    if k % 512:
        return np.exp2(np.random.permutation(np.resize(levels, k // 32))).repeat(32)
    a = np.empty((k // 512, 16))
    for p in range(k // 512):
        a[p, :8] = np.random.permutation(np.resize(levels, 8))
        for g in range(8):
            far = levels[np.abs(levels - a[p, g]) >= 10]
            a[p, g + 8] = far[np.random.randint(len(far))]
    return np.exp2(a.ravel()).repeat(32)


def f64(x):
    return np.asarray(x).astype(np.float64)


def striped(idx):
    return np.tile(idx.reshape(-1, 16).T, (8, 1)).astype(np.uint16)


def unstriped(offs):
    return offs[:16].T.reshape(-1).astype(np.int64)


def striped8(idx):
    return np.concatenate([x.reshape(-1, 16).T for x in idx]).astype(np.uint16)


def runs(offs, k):
    lists = np.stack([offs[16 * r : 16 * r + 16].T.reshape(-1) for r in range(8)]).astype(np.int64)
    return lists[np.arange(k) % 512 // 64]


def pack_weight(w):
    k, n = w.shape
    w = f64(np.asarray(w, np.float32).astype(ml_dtypes.bfloat16)).reshape(k // 32, 32, n)
    amax = np.abs(w).max(1)
    byte = np.clip(np.where(amax > 0, np.frexp(amax)[1] - 1 + 127 - 7, 1), 1, 254)
    scaled = (w * np.exp2(127.0 - byte)[:, None, :]).reshape(k, n).astype(np.float32)
    words = np.ascontiguousarray(scaled.reshape(k // 512, 128, 4, n).transpose(0, 1, 3, 2)).astype(ml_dtypes.float8_e4m3fn).view(np.uint8)
    return words, np.ascontiguousarray(byte.astype(np.uint8).reshape(k // 512, 16, n))


def unpack_weight(words, scales):
    g, p, n, _ = words.shape
    vals = np.ascontiguousarray(words).view(ml_dtypes.float8_e4m3fn).astype(np.float64) * np.repeat(np.exp2(scales.astype(np.float64) - 127.0), 8, axis=1)[..., None]
    return vals.transpose(0, 1, 3, 2).reshape(g * 512, n)

def planes(y):
    n, m = y.shape
    v = y.astype(np.float32).astype(ml_dtypes.bfloat16).astype(np.float64).reshape(n // 32, 32, m)
    top = np.abs(v).max(1)
    byte = np.clip(np.where(top > 0, np.frexp(top)[1] - 1 + 127 - 7, 1), 1, 254)
    codes = (v * np.exp2(127.0 - byte)[:, None, :]).reshape(n, m).astype(np.float32).astype(ml_dtypes.float8_e4m3fn).view(np.uint8)
    words = codes.reshape(n // 512, 128, 4, m).transpose(0, 1, 3, 2)
    return np.ascontiguousarray(words), np.ascontiguousarray(byte.astype(np.uint8).reshape(n // 512, 16, m))


K, T, S, N = 512, 2048, 512, 512


def setup_inputs():
    n = np.random.standard_normal
    s = mx_kscale(K)[:, None]
    packed_xT = pack_weight(n((K, T)) * s)
    return {
        "x_words": packed_xT[0],
        "x_scales": packed_xT[1],
        "w1": (n((K, N)) / np.sqrt(K) / s).astype(np.float32),
        "offs": striped(np.random.permutation(T)[:S]),
        "n1": striped8(np.stack([np.random.permutation(S) for _ in range(8)])),
        "n2": striped8(np.stack([np.random.permutation(S) for _ in range(8)])),
        "n3": striped8(np.stack([np.random.permutation(S) for _ in range(8)])),
    }


def reference(x_words, x_scales, w1, offs, n1, n2, n3):
    xq = unpack_weight(x_words, x_scales)[:, unstriped(offs)]
    y = mxq(f64(w1), 0, "e4m3").T @ xq
    e0 = np.exp(y)
    out_0 = np.log(e0 + e0[np.arange(N)[:, None], runs(n1, N)] + e0[np.arange(N)[:, None], runs(n2, N)] + e0[np.arange(N)[:, None], runs(n3, N)]) - y
    return (out_0,) + planes(out_0)

@@ -1,0 +1,164 @@
+from contextlib import ExitStack
+
+import concourse.mybir as mybir
+
+K, T, S, N = 512, 2048, 512, 512
+FLOPS = 2 * K * N * S
+
+F32 = mybir.dt.float32
+BF16 = mybir.dt.bfloat16
+I32 = mybir.dt.int32
+U32 = mybir.dt.uint32
+U16 = mybir.dt.uint16
+U8 = mybir.dt.uint8
+FP8X4 = mybir.dt.float8_e4m3fn_x4
+ACT = mybir.ActivationFunctionType
+ALU = mybir.AluOpType
+
+P = 128
+PACK = 4
+HALF = S // 2
+M_VECTOR = 64
+J_SCALAR = (128, 80)
+
+
+def tile_picked_nce8_none_po_kernel(
+    tc, x_words, x_scales, w1, offs, n1, n2, n3, out_0, out_1, out_2
+):
+    nc = tc.nc
+    with ExitStack() as ctx:
+        sb = ctx.enter_context(tc.tile_pool(name="sb", bufs=1))
+        ps = ctx.enter_context(tc.psum_pool(name="ps", bufs=1))
+
+        offs_sb = sb.tile([P, S // 16], U16, name="offs_sb")
+        neg_sb = [sb.tile([P, S // 16], U16, name="neg%d" % i) for i in range(3)]
+        w_raw = sb.tile([P, PACK, N], F32, name="w_raw")
+        x_tab = sb.tile([P, T], U32, name="x_tab")
+        xs_tab = sb.tile([P, T], U8, name="xs_tab")
+
+        nc.vector.memset(xs_tab[:].bitcast(I32), 0)
+        nc.sync.dma_start(offs_sb[:], offs)
+        nc.sync.dma_start(neg_sb[0][:], n1)
+        nc.sync.dma_start(w_raw[:], w1.rearrange("(p j) c -> p j c", j=PACK))
+        for q in range(4):
+            nc.scalar.dma_start(
+                xs_tab[32 * q : 32 * q + 4, :].bitcast(I32), x_scales[0, 4 * q : 4 * q + 4, :].bitcast(I32)
+            )
+        nc.sync.dma_start(x_tab[:].bitcast(I32), x_words[0].rearrange("p n t -> p (n t)").bitcast(I32))
+        nc.sync.dma_start(neg_sb[1][:], n2)
+        nc.sync.dma_start(neg_sb[2][:], n3)
+
+        xs = sb.tile([P, S], U8, name="xs", align_bytes=64)
+        nc.vector.tensor_copy(xs[:], xs_tab[:].indirect(offs_sb[:]))
+
+        w_bf = sb.tile([P, PACK * N], BF16, name="w_bf", align_bytes=64)
+        w_dst = w_bf[:].rearrange("p (t m j) -> p m t j", t=PACK, j=PACK)
+        w_src = w_raw[:].rearrange("p j (m t) -> p m t j", t=PACK)
+        nc.vector.tensor_copy(w_dst[:, :M_VECTOR], w_src[:, :M_VECTOR])
+        nc.scalar.copy(w_dst[:, M_VECTOR:], w_src[:, M_VECTOR:])
+        w_codes = sb.tile([P, N], U32, name="w_codes", align_bytes=64)
+        w_scales = sb.tile([P, N], U8, name="w_scales", align_bytes=64)
+        nc.vector.quantize_mx(out=w_codes[:].bitcast(FP8X4), scales=w_scales[:], in_=w_bf[:])
+
+        y_ps = {}
+        for h in range(2):
+            x_codes = sb.tile([P, HALF], U32, name="x_codes%d" % h, align_bytes=64)
+            nc.vector.tensor_copy(x_codes[:], x_tab[:].indirect(offs_sb[:, h * 16 : (h + 1) * 16]))
+            for t in range(PACK):
+                y_ps[t, h] = ps.tile([P, HALF], F32, name="y_ps%d%d" % (t, h))
+                nc.tensor.matmul_mx(
+                    out=y_ps[t, h][:],
+                    lhsT=w_codes[:, t * P : (t + 1) * P].bitcast(FP8X4),
+                    lhsT_scale=w_scales[:, t * P : (t + 1) * P],
+                    rhs=x_codes[:].bitcast(FP8X4),
+                    rhs_scale=xs[:, h * HALF : (h + 1) * HALF],
+                    start=True,
+                    stop=True,
+                )
+
+        def half(h):
+            return slice(h * HALF, (h + 1) * HALF)
+
+        def entries(i, h):
+            return neg_sb[i][:, h * 16 : (h + 1) * 16]
+
+        e = [sb.tile([P, S], F32, name="e%d" % t) for t in range(PACK)]
+        y_sb = {t: sb.tile([P, S], F32, name="y_sb%d" % t) for t in range(1, PACK)}
+        recip = sb.tile([P, PACK, S], F32, name="recip")
+        sums = [[sb.tile([P, PACK, HALF], F32, name="sum%d_%d" % (h, i)) for i in range(3)] for h in range(2)]
+        ratio = [sb.tile([P, PACK, HALF], F32, name="ratio%d" % h) for h in range(2)]
+        loss = [sb.tile([P, PACK, HALF], F32, name="loss%d" % h) for h in range(2)]
+        loss_bf = [sb.tile([P, HALF * PACK], BF16, name="loss_bf%d" % h, align_bytes=64) for h in range(2)]
+        o_codes = [sb.tile([P, HALF], U32, name="o_codes%d" % h, align_bytes=64) for h in range(2)]
+        o_scales = sb.tile([P, S], U8, name="o_scales", align_bytes=64)
+        out_rows = out_0.rearrange("(p t) j -> p t j", t=PACK)
+        out_words = out_1[0].rearrange("p n t -> p (n t)").bitcast(I32)
+
+        def first_negative(t, h):
+            nc.scalar.activation(sums[h][0][:, t, :], y_sb[t][:].indirect(entries(0, h)), ACT.Exp)
+
+        def add_negative(i, t, h):
+            nc.vector.tensor_tensor(
+                sums[h][i][:, t, :], e[t][:].indirect(entries(i, h)), sums[h][i - 1][:, t, :], ALU.add
+            )
+
+        def divide(ts, h):
+            nc.vector.tensor_tensor(ratio[h][:, ts, :], sums[h][2][:, ts, :], recip[:, ts, half(h)], ALU.mult)
+
+        def log_and_store(ts, h):
+            nc.scalar.activation(loss[h][:, ts, :], ratio[h][:, ts, :], ACT.Ln, bias=1.0)
+            nc.sync.dma_start(out_rows[:, ts, half(h)], loss[h][:, ts, :])
+
+        def planes(h):
+            dst = loss_bf[h][:].rearrange("p (c i t) -> p c t i", i=4, t=PACK)
+            src = loss[h][:].rearrange("p t (c i) -> p c t i", i=4)
+            cut = J_SCALAR[h] // 4
+            nc.scalar.copy(dst[:, :cut], src[:, :cut])
+            nc.vector.tensor_copy(dst[:, cut:], src[:, cut:])
+            nc.vector.quantize_mx(out=o_codes[h][:].bitcast(FP8X4), scales=o_scales[:, half(h)], in_=loss_bf[h][:])
+            nc.sync.dma_start(out_words[:, half(h)], o_codes[h][:].bitcast(I32))
+
+        for t in range(1, PACK):
+            nc.vector.tensor_copy(y_sb[t][:, half(0)], y_ps[t, 0][:])
+        for h in range(2):
+            nc.scalar.activation(e[0][:, half(h)], y_ps[0, h][:], ACT.Exp)
+        for h in range(2):
+            nc.vector.tensor_copy(sums[h][0][:, 0, :], e[0][:].indirect(entries(0, h)))
+        for i in (1, 2):
+            for h in range(2):
+                add_negative(i, 0, h)
+
+        for t in range(1, PACK):
+            nc.scalar.copy(y_sb[t][:, half(1)], y_ps[t, 1][:])
+            nc.scalar.activation(e[t][:], y_sb[t][:], ACT.Exp)
+            first_negative(t, 0)
+        for h in range(2):
+            nc.scalar.activation(recip[:, 0, half(h)], y_ps[0, h][:], ACT.Exp, scale=-1.0)
+        for t in range(1, PACK):
+            nc.scalar.activation(recip[:, t, :], y_sb[t][:], ACT.Exp, scale=-1.0)
+        for t in range(1, PACK):
+            first_negative(t, 1)
+
+        every, early, last = slice(0, PACK), slice(0, PACK - 1), slice(PACK - 1, PACK)
+        for i in (1, 2):
+            for t in range(1, PACK):
+                add_negative(i, t, 0)
+        add_negative(1, 1, 1)
+        divide(every, 0)
+        log_and_store(every, 0)
+        add_negative(1, 2, 1)
+        add_negative(1, 3, 1)
+        add_negative(2, 1, 1)
+        add_negative(2, 2, 1)
+        add_negative(2, 3, 1)
+        divide(early, 1)
+        divide(last, 1)
+        log_and_store(early, 1)
+        log_and_store(last, 1)
+        planes(0)
+        planes(1)
+        for q in range(4):
+            queue = nc.scalar if q % 2 else nc.sync
+            queue.dma_start(
+                out_2[0, 4 * q : 4 * q + 4, :].bitcast(I32), o_scales[32 * q : 32 * q + 4, :].bitcast(I32)
+            )

@@ -18,8 +18,8 @@ ALU = mybir.AluOpType
 P = 128
 PACK = 4
 HALF = S // 2
-M_VECTOR = 64
-J_SCALAR = (128, 80)
+M_VECTOR = 40
+J_SCALAR = (256, 96)
 
 
 def tile_picked_nce8_none_po_kernel(
@@ -36,15 +36,16 @@ def tile_picked_nce8_none_po_kernel(
         x_tab = sb.tile([P, T], U32, name="x_tab")
         xs_tab = sb.tile([P, T], U8, name="xs_tab")
 
-        nc.vector.memset(xs_tab[:].bitcast(I32), 0)
+        nc.gpsimd.memset(xs_tab[:].bitcast(I32), 0)
         nc.sync.dma_start(offs_sb[:], offs)
-        nc.sync.dma_start(neg_sb[0][:], n1)
         nc.sync.dma_start(w_raw[:], w1.rearrange("(p j) c -> p j c", j=PACK))
         for q in range(4):
-            nc.scalar.dma_start(
+            queue = nc.gpsimd if q % 2 else nc.scalar
+            queue.dma_start(
                 xs_tab[32 * q : 32 * q + 4, :].bitcast(I32), x_scales[0, 4 * q : 4 * q + 4, :].bitcast(I32)
             )
         nc.sync.dma_start(x_tab[:].bitcast(I32), x_words[0].rearrange("p n t -> p (n t)").bitcast(I32))
+        nc.sync.dma_start(neg_sb[0][:], n1)
         nc.sync.dma_start(neg_sb[1][:], n2)
         nc.sync.dma_start(neg_sb[2][:], n3)
 
@@ -114,7 +115,8 @@ def tile_picked_nce8_none_po_kernel(
             src = loss[h][:].rearrange("p t (c i) -> p c t i", i=4)
             cut = J_SCALAR[h] // 4
             nc.scalar.copy(dst[:, :cut], src[:, :cut])
-            nc.vector.tensor_copy(dst[:, cut:], src[:, cut:])
+            if cut < HALF // 4:
+                nc.vector.tensor_copy(dst[:, cut:], src[:, cut:])
             nc.vector.quantize_mx(out=o_codes[h][:].bitcast(FP8X4), scales=o_scales[:, half(h)], in_=loss_bf[h][:])
             nc.sync.dma_start(out_words[:, half(h)], o_codes[h][:].bitcast(I32))
 
@@ -146,16 +148,16 @@ def tile_picked_nce8_none_po_kernel(
         add_negative(1, 1, 1)
         divide(every, 0)
         log_and_store(every, 0)
+        planes(0)
         add_negative(1, 2, 1)
         add_negative(1, 3, 1)
         add_negative(2, 1, 1)
         add_negative(2, 2, 1)
-        add_negative(2, 3, 1)
         divide(early, 1)
-        divide(last, 1)
         log_and_store(early, 1)
+        add_negative(2, 3, 1)
+        divide(last, 1)
         log_and_store(last, 1)
-        planes(0)
         planes(1)
         for q in range(4):
             queue = nc.scalar if q % 2 else nc.sync

@@ -18,8 +18,8 @@ ALU = mybir.AluOpType
 P = 128
 PACK = 4
 HALF = S // 2
-M_VECTOR = 40
-J_SCALAR = (256, 96)
+M_SCALAR = 80
+J_SCALAR = (0, 160)
 
 
 def tile_picked_nce8_none_po_kernel(
@@ -32,46 +32,48 @@ def tile_picked_nce8_none_po_kernel(
 
         offs_sb = sb.tile([P, S // 16], U16, name="offs_sb")
         neg_sb = [sb.tile([P, S // 16], U16, name="neg%d" % i) for i in range(3)]
-        w_raw = sb.tile([P, PACK, N], F32, name="w_raw")
+        w_left = sb.tile([P, PACK, PACK * M_SCALAR], F32, name="w_left")
+        w_right = sb.tile([P, PACK, N - PACK * M_SCALAR], F32, name="w_right")
         x_tab = sb.tile([P, T], U32, name="x_tab")
         xs_tab = sb.tile([P, T], U8, name="xs_tab")
 
-        nc.gpsimd.memset(xs_tab[:].bitcast(I32), 0)
+        nc.vector.memset(xs_tab[:].bitcast(I32), 0)
         nc.sync.dma_start(offs_sb[:], offs)
-        nc.sync.dma_start(w_raw[:], w1.rearrange("(p j) c -> p j c", j=PACK))
+        nc.sync.dma_start(neg_sb[0][:], n1)
+        nc.sync.dma_start(neg_sb[1][:], n2)
+        w_rows = w1.rearrange("(p j) c -> p j c", j=PACK)
+        nc.sync.dma_start(w_left[:], w_rows[:, :, : PACK * M_SCALAR])
+        nc.sync.dma_start(w_right[:], w_rows[:, :, PACK * M_SCALAR :])
+        nc.sync.dma_start(neg_sb[2][:], n3)
         for q in range(4):
-            queue = nc.gpsimd if q % 2 else nc.scalar
-            queue.dma_start(
+            nc.sync.dma_start(
                 xs_tab[32 * q : 32 * q + 4, :].bitcast(I32), x_scales[0, 4 * q : 4 * q + 4, :].bitcast(I32)
             )
         nc.sync.dma_start(x_tab[:].bitcast(I32), x_words[0].rearrange("p n t -> p (n t)").bitcast(I32))
-        nc.sync.dma_start(neg_sb[0][:], n1)
-        nc.sync.dma_start(neg_sb[1][:], n2)
-        nc.sync.dma_start(neg_sb[2][:], n3)
 
         xs = sb.tile([P, S], U8, name="xs", align_bytes=64)
         nc.vector.tensor_copy(xs[:], xs_tab[:].indirect(offs_sb[:]))
 
         w_bf = sb.tile([P, PACK * N], BF16, name="w_bf", align_bytes=64)
         w_dst = w_bf[:].rearrange("p (t m j) -> p m t j", t=PACK, j=PACK)
-        w_src = w_raw[:].rearrange("p j (m t) -> p m t j", t=PACK)
-        nc.vector.tensor_copy(w_dst[:, :M_VECTOR], w_src[:, :M_VECTOR])
-        nc.scalar.copy(w_dst[:, M_VECTOR:], w_src[:, M_VECTOR:])
+        nc.scalar.copy(w_dst[:, :M_SCALAR], w_left[:].rearrange("p j (m t) -> p m t j", t=PACK))
+        nc.vector.tensor_copy(w_dst[:, M_SCALAR:], w_right[:].rearrange("p j (m t) -> p m t j", t=PACK))
         w_codes = sb.tile([P, N], U32, name="w_codes", align_bytes=64)
         w_scales = sb.tile([P, N], U8, name="w_scales", align_bytes=64)
         nc.vector.quantize_mx(out=w_codes[:].bitcast(FP8X4), scales=w_scales[:], in_=w_bf[:])
 
         y_ps = {}
+        x_codes = [sb.tile([P, HALF], U32, name="x_codes%d" % h, align_bytes=64) for h in range(2)]
         for h in range(2):
-            x_codes = sb.tile([P, HALF], U32, name="x_codes%d" % h, align_bytes=64)
-            nc.vector.tensor_copy(x_codes[:], x_tab[:].indirect(offs_sb[:, h * 16 : (h + 1) * 16]))
-            for t in range(PACK):
+            nc.vector.tensor_copy(x_codes[h][:], x_tab[:].indirect(offs_sb[:, h * 16 : (h + 1) * 16]))
+        for t in range(PACK):
+            for h in range(2):
                 y_ps[t, h] = ps.tile([P, HALF], F32, name="y_ps%d%d" % (t, h))
                 nc.tensor.matmul_mx(
                     out=y_ps[t, h][:],
                     lhsT=w_codes[:, t * P : (t + 1) * P].bitcast(FP8X4),
                     lhsT_scale=w_scales[:, t * P : (t + 1) * P],
-                    rhs=x_codes[:].bitcast(FP8X4),
+                    rhs=x_codes[h][:].bitcast(FP8X4),
                     rhs_scale=xs[:, h * HALF : (h + 1) * HALF],
                     start=True,
                     stop=True,
@@ -95,12 +97,14 @@ def tile_picked_nce8_none_po_kernel(
         out_rows = out_0.rearrange("(p t) j -> p t j", t=PACK)
         out_words = out_1[0].rearrange("p n t -> p (n t)").bitcast(I32)
 
+        second = sb.tile([P, 2, HALF], F32, name="second")
+
         def first_negative(t, h):
             nc.scalar.activation(sums[h][0][:, t, :], y_sb[t][:].indirect(entries(0, h)), ACT.Exp)
 
-        def add_negative(i, t, h):
+        def add_negative(i, t, h, lists=None):
             nc.vector.tensor_tensor(
-                sums[h][i][:, t, :], e[t][:].indirect(entries(i, h)), sums[h][i - 1][:, t, :], ALU.add
+                sums[h][i][:, t, :], e[t][:].indirect(entries(lists or i, h)), sums[h][i - 1][:, t, :], ALU.add
             )
 
         def divide(ts, h):
@@ -114,9 +118,9 @@ def tile_picked_nce8_none_po_kernel(
             dst = loss_bf[h][:].rearrange("p (c i t) -> p c t i", i=4, t=PACK)
             src = loss[h][:].rearrange("p t (c i) -> p c t i", i=4)
             cut = J_SCALAR[h] // 4
-            nc.scalar.copy(dst[:, :cut], src[:, :cut])
-            if cut < HALF // 4:
-                nc.vector.tensor_copy(dst[:, cut:], src[:, cut:])
+            if cut:
+                nc.scalar.copy(dst[:, :cut], src[:, :cut])
+            nc.vector.tensor_copy(dst[:, cut:], src[:, cut:])
             nc.vector.quantize_mx(out=o_codes[h][:].bitcast(FP8X4), scales=o_scales[:, half(h)], in_=loss_bf[h][:])
             nc.sync.dma_start(out_words[:, half(h)], o_codes[h][:].bitcast(I32))
 
@@ -138,26 +142,28 @@ def tile_picked_nce8_none_po_kernel(
             nc.scalar.activation(recip[:, 0, half(h)], y_ps[0, h][:], ACT.Exp, scale=-1.0)
         for t in range(1, PACK):
             nc.scalar.activation(recip[:, t, :], y_sb[t][:], ACT.Exp, scale=-1.0)
-        for t in range(1, PACK):
+        for t in (1, 2):
             first_negative(t, 1)
+        for t in (1, 2):
+            nc.scalar.activation(second[:, t - 1, :], y_sb[t][:].indirect(entries(1, 1)), ACT.Exp)
+        first_negative(3, 1)
 
         every, early, last = slice(0, PACK), slice(0, PACK - 1), slice(PACK - 1, PACK)
         for i in (1, 2):
             for t in range(1, PACK):
                 add_negative(i, t, 0)
-        add_negative(1, 1, 1)
         divide(every, 0)
         log_and_store(every, 0)
-        planes(0)
-        add_negative(1, 2, 1)
+        add_negative(1, 1, 1, 2)
+        add_negative(1, 2, 1, 2)
+        nc.vector.tensor_tensor(sums[1][2][:, 1:3, :], sums[1][1][:, 1:3, :], second[:], ALU.add)
         add_negative(1, 3, 1)
-        add_negative(2, 1, 1)
-        add_negative(2, 2, 1)
         divide(early, 1)
         log_and_store(early, 1)
         add_negative(2, 3, 1)
         divide(last, 1)
         log_and_store(last, 1)
+        planes(0)
         planes(1)
         for q in range(4):
             queue = nc.scalar if q % 2 else nc.sync

@@ -17,9 +17,24 @@ ALU = mybir.AluOpType
 
 P = 128
 PACK = 4
+QUADRANTS = 4
 HALF = S // 2
+LIST_COLS = HALF // 16
 M_SCALAR = 80
-J_SCALAR = (0, 160)
+J_SCALAR = 80
+PRODUCTS = ((0, 0), (1, 0), (0, 1), (2, 0), (3, 0), (1, 1), (2, 1), (3, 1))
+
+
+def half(h):
+    return slice(h * HALF, (h + 1) * HALF)
+
+
+def entries(lists, h):
+    return lists[:, h * LIST_COLS : (h + 1) * LIST_COLS]
+
+
+def scale_rows(q):
+    return slice(32 * q, 32 * q + 4), slice(4 * q, 4 * q + 4)
 
 
 def tile_picked_nce8_none_po_kernel(
@@ -31,142 +46,142 @@ def tile_picked_nce8_none_po_kernel(
         ps = ctx.enter_context(tc.psum_pool(name="ps", bufs=1))
 
         offs_sb = sb.tile([P, S // 16], U16, name="offs_sb")
-        neg_sb = [sb.tile([P, S // 16], U16, name="neg%d" % i) for i in range(3)]
+        n1_sb = sb.tile([P, S // 16], U16, name="n1_sb")
+        n2_sb = sb.tile([P, S // 16], U16, name="n2_sb")
+        n3_sb = sb.tile([P, S // 16], U16, name="n3_sb")
         w_left = sb.tile([P, PACK, PACK * M_SCALAR], F32, name="w_left")
         w_right = sb.tile([P, PACK, N - PACK * M_SCALAR], F32, name="w_right")
-        x_tab = sb.tile([P, T], U32, name="x_tab")
-        xs_tab = sb.tile([P, T], U8, name="xs_tab")
+        x_table = sb.tile([P, T], U32, name="x_table")
+        xs_table = sb.tile([P, T], U8, name="xs_table")
 
-        nc.vector.memset(xs_tab[:].bitcast(I32), 0)
+        nc.vector.memset(xs_table[:].bitcast(I32), 0)
         nc.sync.dma_start(offs_sb[:], offs)
-        nc.sync.dma_start(neg_sb[0][:], n1)
-        nc.sync.dma_start(neg_sb[1][:], n2)
+        nc.sync.dma_start(n1_sb[:], n1)
+        nc.sync.dma_start(n2_sb[:], n2)
         w_rows = w1.rearrange("(p j) c -> p j c", j=PACK)
         nc.sync.dma_start(w_left[:], w_rows[:, :, : PACK * M_SCALAR])
         nc.sync.dma_start(w_right[:], w_rows[:, :, PACK * M_SCALAR :])
-        nc.sync.dma_start(neg_sb[2][:], n3)
-        for q in range(4):
-            nc.sync.dma_start(
-                xs_tab[32 * q : 32 * q + 4, :].bitcast(I32), x_scales[0, 4 * q : 4 * q + 4, :].bitcast(I32)
-            )
-        nc.sync.dma_start(x_tab[:].bitcast(I32), x_words[0].rearrange("p n t -> p (n t)").bitcast(I32))
+        nc.sync.dma_start(n3_sb[:], n3)
+        for q in range(QUADRANTS):
+            partitions, rows = scale_rows(q)
+            nc.sync.dma_start(xs_table[partitions, :].bitcast(I32), x_scales[0, rows, :].bitcast(I32))
+        nc.sync.dma_start(x_table[:].bitcast(I32), x_words[0].rearrange("p n j -> p (n j)").bitcast(I32))
 
-        xs = sb.tile([P, S], U8, name="xs", align_bytes=64)
-        nc.vector.tensor_copy(xs[:], xs_tab[:].indirect(offs_sb[:]))
+        x_picked_scales = sb.tile([P, S], U8, name="x_picked_scales", align_bytes=64)
+        nc.vector.tensor_copy(x_picked_scales[:], xs_table[:].indirect(offs_sb[:]))
 
         w_bf = sb.tile([P, PACK * N], BF16, name="w_bf", align_bytes=64)
-        w_dst = w_bf[:].rearrange("p (t m j) -> p m t j", t=PACK, j=PACK)
-        nc.scalar.copy(w_dst[:, :M_SCALAR], w_left[:].rearrange("p j (m t) -> p m t j", t=PACK))
-        nc.vector.tensor_copy(w_dst[:, M_SCALAR:], w_right[:].rearrange("p j (m t) -> p m t j", t=PACK))
+        w_dealt = w_bf[:].rearrange("p (t m j) -> p m t j", t=PACK, j=PACK)
+        nc.scalar.copy(w_dealt[:, :M_SCALAR], w_left[:].rearrange("p j (m t) -> p m t j", t=PACK))
+        nc.vector.tensor_copy(w_dealt[:, M_SCALAR:], w_right[:].rearrange("p j (m t) -> p m t j", t=PACK))
         w_codes = sb.tile([P, N], U32, name="w_codes", align_bytes=64)
         w_scales = sb.tile([P, N], U8, name="w_scales", align_bytes=64)
         nc.vector.quantize_mx(out=w_codes[:].bitcast(FP8X4), scales=w_scales[:], in_=w_bf[:])
 
-        y_ps = {}
-        x_codes = [sb.tile([P, HALF], U32, name="x_codes%d" % h, align_bytes=64) for h in range(2)]
+        x_picked = [sb.tile([P, HALF], U32, name="x_picked%d" % h, align_bytes=64) for h in range(2)]
         for h in range(2):
-            nc.vector.tensor_copy(x_codes[h][:], x_tab[:].indirect(offs_sb[:, h * 16 : (h + 1) * 16]))
-        for t in range(PACK):
-            for h in range(2):
-                y_ps[t, h] = ps.tile([P, HALF], F32, name="y_ps%d%d" % (t, h))
-                nc.tensor.matmul_mx(
-                    out=y_ps[t, h][:],
-                    lhsT=w_codes[:, t * P : (t + 1) * P].bitcast(FP8X4),
-                    lhsT_scale=w_scales[:, t * P : (t + 1) * P],
-                    rhs=x_codes[h][:].bitcast(FP8X4),
-                    rhs_scale=xs[:, h * HALF : (h + 1) * HALF],
-                    start=True,
-                    stop=True,
-                )
+            nc.vector.tensor_copy(x_picked[h][:], x_table[:].indirect(entries(offs_sb, h)))
 
-        def half(h):
-            return slice(h * HALF, (h + 1) * HALF)
+        y_ps = {}
+        for t, h in PRODUCTS:
+            y_ps[t, h] = ps.tile([P, HALF], F32, name="y_ps%d%d" % (t, h))
+            nc.tensor.matmul_mx(
+                out=y_ps[t, h][:],
+                lhsT=w_codes[:, t * P : (t + 1) * P].bitcast(FP8X4),
+                lhsT_scale=w_scales[:, t * P : (t + 1) * P],
+                rhs=x_picked[h][:].bitcast(FP8X4),
+                rhs_scale=x_picked_scales[:, half(h)],
+                start=True,
+                stop=True,
+            )
 
-        def entries(i, h):
-            return neg_sb[i][:, h * 16 : (h + 1) * 16]
-
-        e = [sb.tile([P, S], F32, name="e%d" % t) for t in range(PACK)]
+        exp_y = [sb.tile([P, S], F32, name="exp_y%d" % t) for t in range(PACK)]
         y_sb = {t: sb.tile([P, S], F32, name="y_sb%d" % t) for t in range(1, PACK)}
-        recip = sb.tile([P, PACK, S], F32, name="recip")
+        exp_neg_y = sb.tile([P, PACK, S], F32, name="exp_neg_y")
         sums = [[sb.tile([P, PACK, HALF], F32, name="sum%d_%d" % (h, i)) for i in range(3)] for h in range(2)]
         ratio = [sb.tile([P, PACK, HALF], F32, name="ratio%d" % h) for h in range(2)]
         loss = [sb.tile([P, PACK, HALF], F32, name="loss%d" % h) for h in range(2)]
         loss_bf = [sb.tile([P, HALF * PACK], BF16, name="loss_bf%d" % h, align_bytes=64) for h in range(2)]
-        o_codes = [sb.tile([P, HALF], U32, name="o_codes%d" % h, align_bytes=64) for h in range(2)]
-        o_scales = sb.tile([P, S], U8, name="o_scales", align_bytes=64)
+        out_codes = [sb.tile([P, HALF], U32, name="out_codes%d" % h, align_bytes=64) for h in range(2)]
+        out_scales = sb.tile([P, S], U8, name="out_scales", align_bytes=64)
         out_rows = out_0.rearrange("(p t) j -> p t j", t=PACK)
-        out_words = out_1[0].rearrange("p n t -> p (n t)").bitcast(I32)
+        out_words = out_1[0].rearrange("p n j -> p (n j)").bitcast(I32)
+        extra = sb.tile([P, 2, HALF], F32, name="extra")
 
-        second = sb.tile([P, 2, HALF], F32, name="second")
+        def scalar_negative(dst, lists, t, h):
+            nc.scalar.activation(dst, y_sb[t][:].indirect(entries(lists, h)), ACT.Exp)
 
-        def first_negative(t, h):
-            nc.scalar.activation(sums[h][0][:, t, :], y_sb[t][:].indirect(entries(0, h)), ACT.Exp)
-
-        def add_negative(i, t, h, lists=None):
+        def add_negative(i, lists, t, h):
             nc.vector.tensor_tensor(
-                sums[h][i][:, t, :], e[t][:].indirect(entries(lists or i, h)), sums[h][i - 1][:, t, :], ALU.add
+                sums[h][i][:, t, :], exp_y[t][:].indirect(entries(lists, h)), sums[h][i - 1][:, t, :], ALU.add
             )
 
-        def divide(ts, h):
-            nc.vector.tensor_tensor(ratio[h][:, ts, :], sums[h][2][:, ts, :], recip[:, ts, half(h)], ALU.mult)
+        def divide(tiles, h):
+            nc.vector.tensor_tensor(ratio[h][:, tiles, :], sums[h][2][:, tiles, :], exp_neg_y[:, tiles, half(h)], ALU.mult)
 
-        def log_and_store(ts, h):
-            nc.scalar.activation(loss[h][:, ts, :], ratio[h][:, ts, :], ACT.Ln, bias=1.0)
-            nc.sync.dma_start(out_rows[:, ts, half(h)], loss[h][:, ts, :])
+        def log_and_store(tiles, h):
+            nc.scalar.activation(loss[h][:, tiles, :], ratio[h][:, tiles, :], ACT.Ln, bias=1.0)
+            nc.sync.dma_start(out_rows[:, tiles, half(h)], loss[h][:, tiles, :])
 
-        def planes(h):
+        def interleaved(h):
             dst = loss_bf[h][:].rearrange("p (c i t) -> p c t i", i=4, t=PACK)
-            src = loss[h][:].rearrange("p t (c i) -> p c t i", i=4)
-            cut = J_SCALAR[h] // 4
-            if cut:
-                nc.scalar.copy(dst[:, :cut], src[:, :cut])
-            nc.vector.tensor_copy(dst[:, cut:], src[:, cut:])
-            nc.vector.quantize_mx(out=o_codes[h][:].bitcast(FP8X4), scales=o_scales[:, half(h)], in_=loss_bf[h][:])
-            nc.sync.dma_start(out_words[:, half(h)], o_codes[h][:].bitcast(I32))
+            return dst, loss[h][:].rearrange("p t (c i) -> p c t i", i=4)
 
-        for t in range(1, PACK):
+        def quantize_and_store(h):
+            nc.vector.quantize_mx(out=out_codes[h][:].bitcast(FP8X4), scales=out_scales[:, half(h)], in_=loss_bf[h][:])
+            nc.sync.dma_start(out_words[:, half(h)], out_codes[h][:].bitcast(I32))
+
+        for t in (1, 2):
             nc.vector.tensor_copy(y_sb[t][:, half(0)], y_ps[t, 0][:])
         for h in range(2):
-            nc.scalar.activation(e[0][:, half(h)], y_ps[0, h][:], ACT.Exp)
+            nc.scalar.activation(exp_y[0][:, half(h)], y_ps[0, h][:], ACT.Exp)
         for h in range(2):
-            nc.vector.tensor_copy(sums[h][0][:, 0, :], e[0][:].indirect(entries(0, h)))
-        for i in (1, 2):
+            nc.vector.tensor_copy(sums[h][0][:, 0, :], exp_y[0][:].indirect(entries(n1_sb, h)))
+        nc.vector.tensor_copy(y_sb[3][:, half(0)], y_ps[3, 0][:])
+        for i, lists in ((1, n2_sb), (2, n3_sb)):
             for h in range(2):
-                add_negative(i, 0, h)
+                add_negative(i, lists, 0, h)
 
         for t in range(1, PACK):
             nc.scalar.copy(y_sb[t][:, half(1)], y_ps[t, 1][:])
-            nc.scalar.activation(e[t][:], y_sb[t][:], ACT.Exp)
-            first_negative(t, 0)
-        for h in range(2):
-            nc.scalar.activation(recip[:, 0, half(h)], y_ps[0, h][:], ACT.Exp, scale=-1.0)
         for t in range(1, PACK):
-            nc.scalar.activation(recip[:, t, :], y_sb[t][:], ACT.Exp, scale=-1.0)
+            nc.scalar.activation(exp_y[t][:], y_sb[t][:], ACT.Exp)
+        for t in range(1, PACK):
+            scalar_negative(sums[0][0][:, t, :], n1_sb, t, 0)
         for t in (1, 2):
-            first_negative(t, 1)
+            scalar_negative(sums[1][0][:, t, :], n1_sb, t, 1)
+        for h in range(2):
+            nc.scalar.activation(exp_neg_y[:, 0, half(h)], y_ps[0, h][:], ACT.Exp, scale=-1.0)
+        for t in range(1, PACK):
+            nc.scalar.activation(exp_neg_y[:, t, :], y_sb[t][:], ACT.Exp, scale=-1.0)
         for t in (1, 2):
-            nc.scalar.activation(second[:, t - 1, :], y_sb[t][:].indirect(entries(1, 1)), ACT.Exp)
-        first_negative(3, 1)
+            scalar_negative(extra[:, t - 1, :], n2_sb, t, 1)
+        scalar_negative(sums[1][0][:, 3, :], n1_sb, 3, 1)
 
         every, early, last = slice(0, PACK), slice(0, PACK - 1), slice(PACK - 1, PACK)
-        for i in (1, 2):
+        for i, lists in ((1, n2_sb), (2, n3_sb)):
             for t in range(1, PACK):
-                add_negative(i, t, 0)
+                add_negative(i, lists, t, 0)
+        for t in (1, 2):
+            add_negative(1, n3_sb, t, 1)
         divide(every, 0)
         log_and_store(every, 0)
-        add_negative(1, 1, 1, 2)
-        add_negative(1, 2, 1, 2)
-        nc.vector.tensor_tensor(sums[1][2][:, 1:3, :], sums[1][1][:, 1:3, :], second[:], ALU.add)
-        add_negative(1, 3, 1)
+        nc.vector.tensor_tensor(sums[1][2][:, 1:3, :], sums[1][1][:, 1:3, :], extra[:], ALU.add)
+        add_negative(1, n2_sb, 3, 1)
         divide(early, 1)
         log_and_store(early, 1)
-        add_negative(2, 3, 1)
+        add_negative(2, n3_sb, 3, 1)
         divide(last, 1)
         log_and_store(last, 1)
-        planes(0)
-        planes(1)
-        for q in range(4):
+
+        dst, src = interleaved(0)
+        nc.vector.tensor_copy(dst, src)
+        quantize_and_store(0)
+        dst, src = interleaved(1)
+        nc.scalar.copy(dst[:, : J_SCALAR // 4], src[:, : J_SCALAR // 4])
+        nc.vector.tensor_copy(dst[:, J_SCALAR // 4 :], src[:, J_SCALAR // 4 :])
+        quantize_and_store(1)
+        for q in range(QUADRANTS):
+            partitions, rows = scale_rows(q)
             queue = nc.scalar if q % 2 else nc.sync
-            queue.dma_start(
-                out_2[0, 4 * q : 4 * q + 4, :].bitcast(I32), o_scales[32 * q : 32 * q + 4, :].bitcast(I32)
-            )
+            queue.dma_start(out_2[0, rows, :].bitcast(I32), out_scales[partitions, :].bitcast(I32))

@@ -20,7 +20,7 @@ PACK = 4
 QUADRANTS = 4
 HALF = S // 2
 LIST_COLS = HALF // 16
-M_SCALAR = 80
+M_SCALAR = 48
 J_SCALAR = 80
 PRODUCTS = ((0, 0), (1, 0), (0, 1), (2, 0), (3, 0), (1, 1), (2, 1), (3, 1))
 
@@ -49,38 +49,41 @@ def tile_picked_nce8_none_po_kernel(
         n1_sb = sb.tile([P, S // 16], U16, name="n1_sb")
         n2_sb = sb.tile([P, S // 16], U16, name="n2_sb")
         n3_sb = sb.tile([P, S // 16], U16, name="n3_sb")
-        w_left = sb.tile([P, PACK, PACK * M_SCALAR], F32, name="w_left")
-        w_right = sb.tile([P, PACK, N - PACK * M_SCALAR], F32, name="w_right")
+        w_raw = sb.tile([P, PACK, N], F32, name="w_raw")
         x_table = sb.tile([P, T], U32, name="x_table")
         xs_table = sb.tile([P, T], U8, name="xs_table")
+        xs_picked = sb.tile([P, S], U8, name="xs_picked")
+        x_picked_scales = sb.tile([P, S], U8, name="x_picked_scales", align_bytes=64)
 
-        nc.vector.memset(xs_table[:].bitcast(I32), 0)
+        nc.vector.memset(xs_table[:, : T // 2].bitcast(I32), 0)
+        nc.gpsimd.memset(xs_table[:, T // 2 :].bitcast(I32), 0)
+        nc.vector.memset(x_picked_scales[:].bitcast(I32), 0)
         nc.sync.dma_start(offs_sb[:], offs)
         nc.sync.dma_start(n1_sb[:], n1)
         nc.sync.dma_start(n2_sb[:], n2)
-        w_rows = w1.rearrange("(p j) c -> p j c", j=PACK)
-        nc.sync.dma_start(w_left[:], w_rows[:, :, : PACK * M_SCALAR])
-        nc.sync.dma_start(w_right[:], w_rows[:, :, PACK * M_SCALAR :])
         nc.sync.dma_start(n3_sb[:], n3)
-        for q in range(QUADRANTS):
-            partitions, rows = scale_rows(q)
-            nc.sync.dma_start(xs_table[partitions, :].bitcast(I32), x_scales[0, rows, :].bitcast(I32))
+        nc.sync.dma_start(xs_table[0:P:8, :].bitcast(I32), x_scales[0].bitcast(I32))
+        nc.sync.dma_start(w_raw[:], w1.rearrange("(p j) c -> p j c", j=PACK))
         nc.sync.dma_start(x_table[:].bitcast(I32), x_words[0].rearrange("p n j -> p (n j)").bitcast(I32))
 
-        x_picked_scales = sb.tile([P, S], U8, name="x_picked_scales", align_bytes=64)
-        nc.vector.tensor_copy(x_picked_scales[:], xs_table[:].indirect(offs_sb[:]))
+        nc.vector.tensor_copy(xs_picked[:], xs_table[:].indirect(offs_sb[:]))
+        for q in range(QUADRANTS):
+            nc.sync.dma_start(
+                x_picked_scales[32 * q : 32 * q + 4, :].bitcast(I32), xs_picked[32 * q : 32 * q + 32 : 8, :].bitcast(I32)
+            )
 
-        w_bf = sb.tile([P, PACK * N], BF16, name="w_bf", align_bytes=64)
+        w_bf = sb.tile([P, PACK * N], BF16, name="w_bf", tag="w_bf", align_bytes=64)
         w_dealt = w_bf[:].rearrange("p (t m j) -> p m t j", t=PACK, j=PACK)
-        nc.scalar.copy(w_dealt[:, :M_SCALAR], w_left[:].rearrange("p j (m t) -> p m t j", t=PACK))
-        nc.vector.tensor_copy(w_dealt[:, M_SCALAR:], w_right[:].rearrange("p j (m t) -> p m t j", t=PACK))
+        w_cols = w_raw[:].rearrange("p j (m t) -> p m t j", t=PACK)
+        nc.scalar.copy(w_dealt[:, :M_SCALAR], w_cols[:, :M_SCALAR])
+        nc.vector.tensor_copy(w_dealt[:, M_SCALAR:], w_cols[:, M_SCALAR:])
         w_codes = sb.tile([P, N], U32, name="w_codes", align_bytes=64)
         w_scales = sb.tile([P, N], U8, name="w_scales", align_bytes=64)
         nc.vector.quantize_mx(out=w_codes[:].bitcast(FP8X4), scales=w_scales[:], in_=w_bf[:])
 
-        x_picked = [sb.tile([P, HALF], U32, name="x_picked%d" % h, align_bytes=64) for h in range(2)]
+        x_picked = sb.tile([P, S], U32, name="x_picked", tag="w_bf", align_bytes=64)
         for h in range(2):
-            nc.vector.tensor_copy(x_picked[h][:], x_table[:].indirect(entries(offs_sb, h)))
+            nc.vector.tensor_copy(x_picked[:, half(h)], x_table[:].indirect(entries(offs_sb, h)))
 
         y_ps = {}
         for t, h in PRODUCTS:
@@ -89,7 +92,7 @@ def tile_picked_nce8_none_po_kernel(
                 out=y_ps[t, h][:],
                 lhsT=w_codes[:, t * P : (t + 1) * P].bitcast(FP8X4),
                 lhsT_scale=w_scales[:, t * P : (t + 1) * P],
-                rhs=x_picked[h][:].bitcast(FP8X4),
+                rhs=x_picked[:, half(h)].bitcast(FP8X4),
                 rhs_scale=x_picked_scales[:, half(h)],
                 start=True,
                 stop=True,

@@ -1,6 +1,7 @@
 from contextlib import ExitStack
 
 import concourse.mybir as mybir
+from concourse.masks import make_identity
 
 K, T, S, N = 512, 2048, 512, 512
 FLOPS = 2 * K * N * S
@@ -20,8 +21,8 @@ PACK = 4
 QUADRANTS = 4
 HALF = S // 2
 LIST_COLS = HALF // 16
-M_SCALAR = 48
-J_SCALAR = 80
+M_SCALAR = 80
+J_SCALAR = 192
 PRODUCTS = ((0, 0), (1, 0), (0, 1), (2, 0), (3, 0), (1, 1), (2, 1), (3, 1))
 
 
@@ -49,141 +50,153 @@ def tile_picked_nce8_none_po_kernel(
         n1_sb = sb.tile([P, S // 16], U16, name="n1_sb")
         n2_sb = sb.tile([P, S // 16], U16, name="n2_sb")
         n3_sb = sb.tile([P, S // 16], U16, name="n3_sb")
-        w_raw = sb.tile([P, PACK, N], F32, name="w_raw")
+        w_left = sb.tile([P, PACK, PACK * M_SCALAR], F32, name="w_left")
+        w_right = sb.tile([P, PACK, N - PACK * M_SCALAR], F32, name="w_right")
         x_table = sb.tile([P, T], U32, name="x_table")
         xs_table = sb.tile([P, T], U8, name="xs_table")
-        xs_picked = sb.tile([P, S], U8, name="xs_picked")
-        x_picked_scales = sb.tile([P, S], U8, name="x_picked_scales", align_bytes=64)
 
-        nc.vector.memset(xs_table[:, : T // 2].bitcast(I32), 0)
-        nc.gpsimd.memset(xs_table[:, T // 2 :].bitcast(I32), 0)
-        nc.vector.memset(x_picked_scales[:].bitcast(I32), 0)
+        nc.vector.memset(xs_table[:].bitcast(I32), 0)
         nc.sync.dma_start(offs_sb[:], offs)
         nc.sync.dma_start(n1_sb[:], n1)
         nc.sync.dma_start(n2_sb[:], n2)
+        w_rows = w1.rearrange("(p j) c -> p j c", j=PACK)
+        nc.sync.dma_start(w_left[:], w_rows[:, :, : PACK * M_SCALAR])
+        nc.sync.dma_start(w_right[:], w_rows[:, :, PACK * M_SCALAR :])
         nc.sync.dma_start(n3_sb[:], n3)
-        nc.sync.dma_start(xs_table[0:P:8, :].bitcast(I32), x_scales[0].bitcast(I32))
-        nc.sync.dma_start(w_raw[:], w1.rearrange("(p j) c -> p j c", j=PACK))
+        for q in range(QUADRANTS):
+            partitions, rows = scale_rows(q)
+            nc.sync.dma_start(xs_table[partitions, :].bitcast(I32), x_scales[0, rows, :].bitcast(I32))
         nc.sync.dma_start(x_table[:].bitcast(I32), x_words[0].rearrange("p n j -> p (n j)").bitcast(I32))
 
-        nc.vector.tensor_copy(xs_picked[:], xs_table[:].indirect(offs_sb[:]))
-        for q in range(QUADRANTS):
-            nc.sync.dma_start(
-                x_picked_scales[32 * q : 32 * q + 4, :].bitcast(I32), xs_picked[32 * q : 32 * q + 32 : 8, :].bitcast(I32)
-            )
+        x_picked_scales = sb.tile([P, S], U8, name="x_picked_scales", align_bytes=64)
+        nc.vector.tensor_copy(x_picked_scales[:], xs_table[:].indirect(offs_sb[:]))
 
-        w_bf = sb.tile([P, PACK * N], BF16, name="w_bf", tag="w_bf", align_bytes=64)
+        w_bf = sb.tile([P, PACK * N], BF16, name="w_bf", align_bytes=64)
         w_dealt = w_bf[:].rearrange("p (t m j) -> p m t j", t=PACK, j=PACK)
-        w_cols = w_raw[:].rearrange("p j (m t) -> p m t j", t=PACK)
-        nc.scalar.copy(w_dealt[:, :M_SCALAR], w_cols[:, :M_SCALAR])
-        nc.vector.tensor_copy(w_dealt[:, M_SCALAR:], w_cols[:, M_SCALAR:])
+        nc.scalar.copy(w_dealt[:, :M_SCALAR], w_left[:].rearrange("p j (m t) -> p m t j", t=PACK))
+        nc.vector.tensor_copy(w_dealt[:, M_SCALAR:], w_right[:].rearrange("p j (m t) -> p m t j", t=PACK))
         w_codes = sb.tile([P, N], U32, name="w_codes", align_bytes=64)
         w_scales = sb.tile([P, N], U8, name="w_scales", align_bytes=64)
         nc.vector.quantize_mx(out=w_codes[:].bitcast(FP8X4), scales=w_scales[:], in_=w_bf[:])
 
-        x_picked = sb.tile([P, S], U32, name="x_picked", tag="w_bf", align_bytes=64)
+        x_picked = sb.tile([P, S], U32, name="x_picked", align_bytes=64)
         for h in range(2):
             nc.vector.tensor_copy(x_picked[:, half(h)], x_table[:].indirect(entries(offs_sb, h)))
 
-        y_ps = {}
-        for t, h in PRODUCTS:
-            y_ps[t, h] = ps.tile([P, HALF], F32, name="y_ps%d%d" % (t, h))
+        ident = sb.tile([P, P], F32, name="ident")
+        make_identity(nc, ident[:])
+
+        def product(out, t, cols):
             nc.tensor.matmul_mx(
-                out=y_ps[t, h][:],
+                out=out,
                 lhsT=w_codes[:, t * P : (t + 1) * P].bitcast(FP8X4),
                 lhsT_scale=w_scales[:, t * P : (t + 1) * P],
-                rhs=x_picked[:, half(h)].bitcast(FP8X4),
-                rhs_scale=x_picked_scales[:, half(h)],
+                rhs=x_picked[:, cols].bitcast(FP8X4),
+                rhs_scale=x_picked_scales[:, cols],
                 start=True,
                 stop=True,
             )
 
-        exp_y = [sb.tile([P, S], F32, name="exp_y%d" % t) for t in range(PACK)]
-        y_sb = {t: sb.tile([P, S], F32, name="y_sb%d" % t) for t in range(1, PACK)}
-        exp_neg_y = sb.tile([P, PACK, S], F32, name="exp_neg_y")
-        sums = [[sb.tile([P, PACK, HALF], F32, name="sum%d_%d" % (h, i)) for i in range(3)] for h in range(2)]
-        ratio = [sb.tile([P, PACK, HALF], F32, name="ratio%d" % h) for h in range(2)]
-        loss = [sb.tile([P, PACK, HALF], F32, name="loss%d" % h) for h in range(2)]
+        y_half = {}
+        for h in range(2):
+            for t in range(2):
+                y_half[t, h] = ps.tile([P, HALF], F32, name="y_half%d%d" % (t, h), tag="bank%d%d" % (t, h))
+                product(y_half[t, h][:], t, half(h))
+        y_ps = {}
+        for t in (2, 3):
+            y_ps[t] = ps.tile([P, S], F32, name="y_ps%d" % t)
+            product(y_ps[t][:], t, slice(0, S))
+
+        exp_y = [sb.tile([P, 2 * S], F32, name="exp_y%d" % t) for t in range(PACK)]
+        y_sb = [sb.tile([P, 2 * S], F32, name="y_sb%d" % t) for t in range(2)]
+        own = {t: sb.tile([P, S], F32, name="own%d" % t) for t in (2, 3)}
+        neg = {(t, i): sb.tile([P, S], F32, name="neg%d%d" % (t, i)) for t in range(PACK) for i in range(3)}
+        lists = (n1_sb, n2_sb, n3_sb)
+        sum_t = [ps.tile([P, S], F32, name="sum_t%d" % t) for t in range(2)]
+        log_sum = [sb.tile([P, S], F32, name="log_sum%d" % t) for t in range(PACK)]
+        loss = sb.tile([P, PACK, S], F32, name="loss")
         loss_bf = [sb.tile([P, HALF * PACK], BF16, name="loss_bf%d" % h, align_bytes=64) for h in range(2)]
         out_codes = [sb.tile([P, HALF], U32, name="out_codes%d" % h, align_bytes=64) for h in range(2)]
         out_scales = sb.tile([P, S], U8, name="out_scales", align_bytes=64)
         out_rows = out_0.rearrange("(p t) j -> p t j", t=PACK)
         out_words = out_1[0].rearrange("p n j -> p (n j)").bitcast(I32)
-        extra = sb.tile([P, 2, HALF], F32, name="extra")
 
-        def scalar_negative(dst, lists, t, h):
-            nc.scalar.activation(dst, y_sb[t][:].indirect(entries(lists, h)), ACT.Exp)
+        def block(b):
+            return slice(b * P, (b + 1) * P)
 
-        def add_negative(i, lists, t, h):
-            nc.vector.tensor_tensor(
-                sums[h][i][:, t, :], exp_y[t][:].indirect(entries(lists, h)), sums[h][i - 1][:, t, :], ALU.add
-            )
+        def scalar_negative(t, i):
+            nc.scalar.activation(neg[t, i][:], y_sb[t][:].indirect(lists[i][:]), ACT.Exp)
 
-        def divide(tiles, h):
-            nc.vector.tensor_tensor(ratio[h][:, tiles, :], sums[h][2][:, tiles, :], exp_neg_y[:, tiles, half(h)], ALU.mult)
+        def add_negative(t, i, to):
+            nc.vector.tensor_tensor(neg[t, i][:], exp_y[t][:].indirect(lists[i][:]), to[:], ALU.add)
 
-        def log_and_store(tiles, h):
-            nc.scalar.activation(loss[h][:, tiles, :], ratio[h][:, tiles, :], ACT.Ln, bias=1.0)
-            nc.sync.dma_start(out_rows[:, tiles, half(h)], loss[h][:, tiles, :])
+        def add_transposed(t, term, first=False, last=False):
+            for b in range(PACK):
+                nc.tensor.matmul(
+                    sum_t[t][:, block(b)], term[:, block(b)], ident[:], is_transpose=True,
+                    start=first and b == 0, stop=last and b == PACK - 1,
+                )
 
         def interleaved(h):
             dst = loss_bf[h][:].rearrange("p (c i t) -> p c t i", i=4, t=PACK)
-            return dst, loss[h][:].rearrange("p t (c i) -> p c t i", i=4)
+            return dst, loss[:, :, half(h)].rearrange("p t (c i) -> p c t i", i=4)
 
         def quantize_and_store(h):
             nc.vector.quantize_mx(out=out_codes[h][:].bitcast(FP8X4), scales=out_scales[:, half(h)], in_=loss_bf[h][:])
             nc.sync.dma_start(out_words[:, half(h)], out_codes[h][:].bitcast(I32))
 
-        for t in (1, 2):
-            nc.vector.tensor_copy(y_sb[t][:, half(0)], y_ps[t, 0][:])
-        for h in range(2):
-            nc.scalar.activation(exp_y[0][:, half(h)], y_ps[0, h][:], ACT.Exp)
-        for h in range(2):
-            nc.vector.tensor_copy(sums[h][0][:, 0, :], exp_y[0][:].indirect(entries(n1_sb, h)))
-        nc.vector.tensor_copy(y_sb[3][:, half(0)], y_ps[3, 0][:])
-        for i, lists in ((1, n2_sb), (2, n3_sb)):
-            for h in range(2):
-                add_negative(i, lists, 0, h)
+        def first_negative(t, i):
+            nc.vector.tensor_copy(neg[t, i][:], exp_y[t][:].indirect(lists[i][:]))
 
-        for t in range(1, PACK):
-            nc.scalar.copy(y_sb[t][:, half(1)], y_ps[t, 1][:])
-        for t in range(1, PACK):
-            nc.scalar.activation(exp_y[t][:], y_sb[t][:], ACT.Exp)
-        for t in range(1, PACK):
-            scalar_negative(sums[0][0][:, t, :], n1_sb, t, 0)
-        for t in (1, 2):
-            scalar_negative(sums[1][0][:, t, :], n1_sb, t, 1)
+        nc.vector.tensor_copy(y_sb[1][:, half(0)], y_half[1, 0][:])
         for h in range(2):
-            nc.scalar.activation(exp_neg_y[:, 0, half(h)], y_ps[0, h][:], ACT.Exp, scale=-1.0)
-        for t in range(1, PACK):
-            nc.scalar.activation(exp_neg_y[:, t, :], y_sb[t][:], ACT.Exp, scale=-1.0)
-        for t in (1, 2):
-            scalar_negative(extra[:, t - 1, :], n2_sb, t, 1)
-        scalar_negative(sums[1][0][:, 3, :], n1_sb, 3, 1)
+            nc.scalar.activation(exp_y[0][:, half(h)], y_half[0, h][:], ACT.Exp)
+        nc.vector.tensor_copy(y_sb[0][:, half(0)], y_half[0, 0][:])
+        nc.scalar.copy(y_sb[1][:, half(1)], y_half[1, 1][:])
+        first_negative(0, 1)
+        nc.scalar.activation(exp_y[2][:, :S], y_ps[2][:], ACT.Exp)
+        add_transposed(0, exp_y[0], first=True)
+        nc.vector.tensor_copy(y_sb[0][:, half(1)], y_half[0, 1][:])
+        scalar_negative(1, 0)
+        add_negative(0, 2, neg[0, 1])
+        nc.scalar.activation(exp_y[3][:, :S], y_ps[3][:], ACT.Exp)
+        add_transposed(1, neg[1, 0], first=True)
+        add_transposed(0, neg[0, 2])
+        for t in (2, 3):
+            first_negative(t, 0)
+        scalar_negative(1, 1)
+        add_transposed(1, neg[1, 1])
+        scalar_negative(1, 2)
+        add_transposed(1, neg[1, 2])
+        nc.scalar.activation(exp_y[1][:, :S], y_sb[1][:, :S], ACT.Exp)
+        add_transposed(1, exp_y[1], last=True)
+        scalar_negative(0, 0)
+        add_transposed(0, neg[0, 0], last=True)
+        for i in (1, 2):
+            for t in (2, 3):
+                add_negative(t, i, neg[t, i - 1])
+        for t in (2, 3):
+            nc.scalar.activation(own[t][:], y_ps[t][:], ACT.Exp, scale=-1.0)
+            nc.vector.tensor_tensor(log_sum[t][:], neg[t, 2][:], own[t][:], ALU.mult)
 
-        every, early, last = slice(0, PACK), slice(0, PACK - 1), slice(PACK - 1, PACK)
-        for i, lists in ((1, n2_sb), (2, n3_sb)):
-            for t in range(1, PACK):
-                add_negative(i, lists, t, 0)
-        for t in (1, 2):
-            add_negative(1, n3_sb, t, 1)
-        divide(every, 0)
-        log_and_store(every, 0)
-        nc.vector.tensor_tensor(sums[1][2][:, 1:3, :], sums[1][1][:, 1:3, :], extra[:], ALU.add)
-        add_negative(1, n2_sb, 3, 1)
-        divide(early, 1)
-        log_and_store(early, 1)
-        add_negative(2, n3_sb, 3, 1)
-        divide(last, 1)
-        log_and_store(last, 1)
+        for t in (1, 0):
+            nc.scalar.activation(log_sum[t][:], sum_t[t][:], ACT.Ln)
+            back = ps.tile([P, S], F32, name="back%d" % t, tag="bank%d0" % t)
+            for b in range(PACK):
+                nc.tensor.transpose(back[:, block(b)], log_sum[t][:, block(b)], ident[:])
+            nc.vector.tensor_tensor(loss[:, t, :], back[:], y_sb[t][:, :S], ALU.subtract)
+            nc.sync.dma_start(out_rows[:, t, :], loss[:, t, :])
+        for t in (2, 3):
+            nc.scalar.activation(loss[:, t, :], log_sum[t][:], ACT.Ln, bias=1.0)
+            nc.sync.dma_start(out_rows[:, t, :], loss[:, t, :])
 
         dst, src = interleaved(0)
-        nc.vector.tensor_copy(dst, src)
-        quantize_and_store(0)
-        dst, src = interleaved(1)
         nc.scalar.copy(dst[:, : J_SCALAR // 4], src[:, : J_SCALAR // 4])
+        dst1, src1 = interleaved(1)
+        nc.vector.tensor_copy(dst1, src1)
         nc.vector.tensor_copy(dst[:, J_SCALAR // 4 :], src[:, J_SCALAR // 4 :])
         quantize_and_store(1)
+        quantize_and_store(0)
         for q in range(QUADRANTS):
             partitions, rows = scale_rows(q)
             queue = nc.scalar if q % 2 else nc.sync

@@ -21,8 +21,8 @@ PACK = 4
 QUADRANTS = 4
 HALF = S // 2
 LIST_COLS = HALF // 16
-M_SCALAR = 80
-J_SCALAR = 192
+M_SCALAR = 48
+J_SCALAR = 96
 PRODUCTS = ((0, 0), (1, 0), (0, 1), (2, 0), (3, 0), (1, 1), (2, 1), (3, 1))
 
 
@@ -50,36 +50,34 @@ def tile_picked_nce8_none_po_kernel(
         n1_sb = sb.tile([P, S // 16], U16, name="n1_sb")
         n2_sb = sb.tile([P, S // 16], U16, name="n2_sb")
         n3_sb = sb.tile([P, S // 16], U16, name="n3_sb")
-        w_left = sb.tile([P, PACK, PACK * M_SCALAR], F32, name="w_left")
-        w_right = sb.tile([P, PACK, N - PACK * M_SCALAR], F32, name="w_right")
+        w_raw = sb.tile([P, PACK, N], F32, name="w_raw")
         x_table = sb.tile([P, T], U32, name="x_table")
         xs_table = sb.tile([P, T], U8, name="xs_table")
 
-        nc.vector.memset(xs_table[:].bitcast(I32), 0)
+        nc.vector.memset(xs_table[:, : T // 2].bitcast(I32), 0)
+        nc.gpsimd.memset(xs_table[:, T // 2 :].bitcast(I32), 0)
         nc.sync.dma_start(offs_sb[:], offs)
         nc.sync.dma_start(n1_sb[:], n1)
         nc.sync.dma_start(n2_sb[:], n2)
-        w_rows = w1.rearrange("(p j) c -> p j c", j=PACK)
-        nc.sync.dma_start(w_left[:], w_rows[:, :, : PACK * M_SCALAR])
-        nc.sync.dma_start(w_right[:], w_rows[:, :, PACK * M_SCALAR :])
-        nc.sync.dma_start(n3_sb[:], n3)
+        nc.sync.dma_start(w_raw[:], w1.rearrange("(p j) c -> p j c", j=PACK))
         for q in range(QUADRANTS):
             partitions, rows = scale_rows(q)
             nc.sync.dma_start(xs_table[partitions, :].bitcast(I32), x_scales[0, rows, :].bitcast(I32))
         nc.sync.dma_start(x_table[:].bitcast(I32), x_words[0].rearrange("p n j -> p (n j)").bitcast(I32))
+        nc.sync.dma_start(n3_sb[:], n3)
 
+        w_bf = sb.tile([P, PACK * N], BF16, name="w_bf", tag="w_bf", align_bytes=64)
+        w_dealt = w_bf[:].rearrange("p (t m j) -> p m t j", t=PACK, j=PACK)
+        w_cols = w_raw[:].rearrange("p j (m t) -> p m t j", t=PACK)
+        nc.scalar.copy(w_dealt[:, :M_SCALAR], w_cols[:, :M_SCALAR])
+        nc.vector.tensor_copy(w_dealt[:, M_SCALAR:], w_cols[:, M_SCALAR:])
         x_picked_scales = sb.tile([P, S], U8, name="x_picked_scales", align_bytes=64)
         nc.vector.tensor_copy(x_picked_scales[:], xs_table[:].indirect(offs_sb[:]))
-
-        w_bf = sb.tile([P, PACK * N], BF16, name="w_bf", align_bytes=64)
-        w_dealt = w_bf[:].rearrange("p (t m j) -> p m t j", t=PACK, j=PACK)
-        nc.scalar.copy(w_dealt[:, :M_SCALAR], w_left[:].rearrange("p j (m t) -> p m t j", t=PACK))
-        nc.vector.tensor_copy(w_dealt[:, M_SCALAR:], w_right[:].rearrange("p j (m t) -> p m t j", t=PACK))
         w_codes = sb.tile([P, N], U32, name="w_codes", align_bytes=64)
         w_scales = sb.tile([P, N], U8, name="w_scales", align_bytes=64)
         nc.vector.quantize_mx(out=w_codes[:].bitcast(FP8X4), scales=w_scales[:], in_=w_bf[:])
 
-        x_picked = sb.tile([P, S], U32, name="x_picked", align_bytes=64)
+        x_picked = sb.tile([P, S], U32, name="x_picked", tag="w_bf", align_bytes=64)
         for h in range(2):
             nc.vector.tensor_copy(x_picked[:, half(h)], x_table[:].indirect(entries(offs_sb, h)))
 
@@ -108,18 +106,23 @@ def tile_picked_nce8_none_po_kernel(
             product(y_ps[t][:], t, slice(0, S))
 
         exp_y = [sb.tile([P, 2 * S], F32, name="exp_y%d" % t) for t in range(PACK)]
-        y_sb = [sb.tile([P, 2 * S], F32, name="y_sb%d" % t) for t in range(2)]
-        own = {t: sb.tile([P, S], F32, name="own%d" % t) for t in (2, 3)}
+        y_sb = {t: sb.tile([P, 2 * S], F32, name="y_sb%d" % t) for t in (1, 3)}
+        own = {t: sb.tile([P, S], F32, name="own%d" % t) for t in (0, 2)}
         neg = {(t, i): sb.tile([P, S], F32, name="neg%d%d" % (t, i)) for t in range(PACK) for i in range(3)}
         lists = (n1_sb, n2_sb, n3_sb)
-        sum_t = [ps.tile([P, S], F32, name="sum_t%d" % t) for t in range(2)]
+        sum_t = {t: ps.tile([P, S], F32, name="sum_t%d" % t) for t in (1, 3)}
         log_sum = [sb.tile([P, S], F32, name="log_sum%d" % t) for t in range(PACK)]
         loss = sb.tile([P, PACK, S], F32, name="loss")
         loss_bf = [sb.tile([P, HALF * PACK], BF16, name="loss_bf%d" % h, align_bytes=64) for h in range(2)]
-        out_codes = [sb.tile([P, HALF], U32, name="out_codes%d" % h, align_bytes=64) for h in range(2)]
+        out_codes = sb.tile([P, S], U32, name="out_codes", align_bytes=64)
         out_scales = sb.tile([P, S], U8, name="out_scales", align_bytes=64)
         out_rows = out_0.rearrange("(p t) j -> p t j", t=PACK)
         out_words = out_1[0].rearrange("p n j -> p (n j)").bitcast(I32)
+
+        ratio = sb.tile([P, 2, S], F32, name="ratio")
+        neg[2, 0] = log_sum[0] = ratio[:, 0, :]
+        neg[3, 2] = log_sum[2] = ratio[:, 1, :]
+        neg[2, 2] = exp_y[3][:, S:]
 
         def block(b):
             return slice(b * P, (b + 1) * P)
@@ -142,61 +145,86 @@ def tile_picked_nce8_none_po_kernel(
             return dst, loss[:, :, half(h)].rearrange("p t (c i) -> p c t i", i=4)
 
         def quantize_and_store(h):
-            nc.vector.quantize_mx(out=out_codes[h][:].bitcast(FP8X4), scales=out_scales[:, half(h)], in_=loss_bf[h][:])
-            nc.sync.dma_start(out_words[:, half(h)], out_codes[h][:].bitcast(I32))
+            nc.vector.quantize_mx(out=out_codes[:, half(h)].bitcast(FP8X4), scales=out_scales[:, half(h)], in_=loss_bf[h][:])
 
         def first_negative(t, i):
             nc.vector.tensor_copy(neg[t, i][:], exp_y[t][:].indirect(lists[i][:]))
 
+        def divide(t, cols):
+            nc.gpsimd.tensor_tensor(log_sum[t][:, cols], neg[t, 2][:, cols], own[t][:, cols], ALU.mult)
+
+        def log_and_store(t, parts):
+            for cols in parts:
+                nc.scalar.activation(loss[:, t, cols], log_sum[t][:, cols], ACT.Ln, bias=1.0)
+            nc.sync.dma_start(out_rows[:, t, :], loss[:, t, :])
+
+        def log_turn_back_and_store(t, banks):
+            for h in range(2):
+                nc.scalar.activation(log_sum[t][:, half(h)], sum_t[t][:, half(h)], ACT.Ln)
+                back = ps.tile([P, HALF], F32, name="back%d%d" % (t, h), tag=banks[h])
+                for b in range(2):
+                    nc.tensor.transpose(back[:, block(b)], log_sum[t][:, block(2 * h + b)], ident[:])
+                nc.vector.tensor_tensor(loss[:, t, half(h)], back[:], y_sb[t][:, half(h)], ALU.subtract)
+            nc.sync.dma_start(out_rows[:, t, :], loss[:, t, :])
+
+        def chain(t, i):
+            for h in range(2):
+                looked_up = exp_y[t][:].indirect(entries(lists[i], h))
+                if i == 0:
+                    nc.vector.tensor_copy(neg[t, i][:, half(h)], looked_up)
+                else:
+                    nc.vector.tensor_tensor(neg[t, i][:, half(h)], looked_up, neg[t, i - 1][:, half(h)], ALU.add)
+
+        whole = slice(0, S)
         nc.vector.tensor_copy(y_sb[1][:, half(0)], y_half[1, 0][:])
         for h in range(2):
             nc.scalar.activation(exp_y[0][:, half(h)], y_half[0, h][:], ACT.Exp)
-        nc.vector.tensor_copy(y_sb[0][:, half(0)], y_half[0, 0][:])
-        nc.scalar.copy(y_sb[1][:, half(1)], y_half[1, 1][:])
-        first_negative(0, 1)
+        nc.vector.tensor_copy(y_sb[1][:, half(1)], y_half[1, 1][:])
         nc.scalar.activation(exp_y[2][:, :S], y_ps[2][:], ACT.Exp)
-        add_transposed(0, exp_y[0], first=True)
-        nc.vector.tensor_copy(y_sb[0][:, half(1)], y_half[0, 1][:])
+        for i in range(3):
+            chain(0, i)
         scalar_negative(1, 0)
-        add_negative(0, 2, neg[0, 1])
-        nc.scalar.activation(exp_y[3][:, :S], y_ps[3][:], ACT.Exp)
         add_transposed(1, neg[1, 0], first=True)
-        add_transposed(0, neg[0, 2])
-        for t in (2, 3):
-            first_negative(t, 0)
+        nc.scalar.activation(exp_y[3][:, :S], y_ps[3][:], ACT.Exp)
+        add_transposed(3, exp_y[3], first=True)
+        nc.vector.tensor_copy(y_sb[3][:, half(0)], y_ps[3][:, half(0)])
+        nc.scalar.copy(y_sb[3][:, half(1)], y_ps[3][:, half(1)])
+        for h in range(2):
+            nc.scalar.activation(own[0][:, half(h)], y_half[0, h][:], ACT.Exp, scale=-1.0)
+        for i in range(2):
+            chain(2, i)
+        divide(0, whole)
+        first_negative(3, 1)
+        first_negative(3, 2)
+        add_negative(2, 2, neg[2, 1])
         scalar_negative(1, 1)
         add_transposed(1, neg[1, 1])
         scalar_negative(1, 2)
         add_transposed(1, neg[1, 2])
         nc.scalar.activation(exp_y[1][:, :S], y_sb[1][:, :S], ACT.Exp)
         add_transposed(1, exp_y[1], last=True)
-        scalar_negative(0, 0)
-        add_transposed(0, neg[0, 0], last=True)
-        for i in (1, 2):
-            for t in (2, 3):
-                add_negative(t, i, neg[t, i - 1])
-        for t in (2, 3):
-            nc.scalar.activation(own[t][:], y_ps[t][:], ACT.Exp, scale=-1.0)
-            nc.vector.tensor_tensor(log_sum[t][:], neg[t, 2][:], own[t][:], ALU.mult)
+        scalar_negative(3, 0)
+        add_transposed(3, neg[3, 0])
+        add_transposed(3, neg[3, 1])
+        add_transposed(3, neg[3, 2], last=True)
+        nc.scalar.activation(own[2][:], y_ps[2][:], ACT.Exp, scale=-1.0)
+        for h in range(2):
+            divide(2, half(h))
 
-        for t in (1, 0):
-            nc.scalar.activation(log_sum[t][:], sum_t[t][:], ACT.Ln)
-            back = ps.tile([P, S], F32, name="back%d" % t, tag="bank%d0" % t)
-            for b in range(PACK):
-                nc.tensor.transpose(back[:, block(b)], log_sum[t][:, block(b)], ident[:])
-            nc.vector.tensor_tensor(loss[:, t, :], back[:], y_sb[t][:, :S], ALU.subtract)
-            nc.sync.dma_start(out_rows[:, t, :], loss[:, t, :])
-        for t in (2, 3):
-            nc.scalar.activation(loss[:, t, :], log_sum[t][:], ACT.Ln, bias=1.0)
-            nc.sync.dma_start(out_rows[:, t, :], loss[:, t, :])
+        log_turn_back_and_store(1, ("bank00", "bank01"))
+        log_turn_back_and_store(3, ("bank10", "bank11"))
+        for h in range(2):
+            nc.scalar.activation(loss[:, 0:PACK:2, half(h)], ratio[:, :, half(h)], ACT.Ln, bias=1.0)
+            nc.sync.dma_start(out_rows[:, 0:PACK:2, half(h)], loss[:, 0:PACK:2, half(h)])
 
         dst, src = interleaved(0)
+        nc.vector.tensor_copy(dst, src)
+        dst, src = interleaved(1)
         nc.scalar.copy(dst[:, : J_SCALAR // 4], src[:, : J_SCALAR // 4])
-        dst1, src1 = interleaved(1)
-        nc.vector.tensor_copy(dst1, src1)
         nc.vector.tensor_copy(dst[:, J_SCALAR // 4 :], src[:, J_SCALAR // 4 :])
-        quantize_and_store(1)
         quantize_and_store(0)
+        quantize_and_store(1)
+        nc.sync.dma_start(out_words, out_codes[:].bitcast(I32))
         for q in range(QUADRANTS):
             partitions, rows = scale_rows(q)
             queue = nc.scalar if q % 2 else nc.sync

@@ -187,8 +187,7 @@ def tile_picked_nce8_none_po_kernel(
         add_transposed(1, neg[1, 0], first=True)
         nc.scalar.activation(exp_y[3][:, :S], y_ps[3][:], ACT.Exp)
         add_transposed(3, exp_y[3], first=True)
-        nc.vector.tensor_copy(y_sb[3][:, half(0)], y_ps[3][:, half(0)])
-        nc.scalar.copy(y_sb[3][:, half(1)], y_ps[3][:, half(1)])
+        nc.scalar.copy(y_sb[3][:, :S], y_ps[3][:])
         for h in range(2):
             nc.scalar.activation(own[0][:, half(h)], y_half[0, h][:], ACT.Exp, scale=-1.0)
         for i in range(2):

@@ -21,13 +21,17 @@ PACK = 4
 QUADRANTS = 4
 HALF = S // 2
 LIST_COLS = HALF // 16
+BLOCKS = S // P
 M_SCALAR = 48
-J_SCALAR = 96
-PRODUCTS = ((0, 0), (1, 0), (0, 1), (2, 0), (3, 0), (1, 1), (2, 1), (3, 1))
+J_SCALAR = 128
 
 
 def half(h):
     return slice(h * HALF, (h + 1) * HALF)
+
+
+def block(b):
+    return slice(b * P, (b + 1) * P)
 
 
 def entries(lists, h):
@@ -66,7 +70,7 @@ def tile_picked_nce8_none_po_kernel(
         nc.sync.dma_start(x_table[:].bitcast(I32), x_words[0].rearrange("p n j -> p (n j)").bitcast(I32))
         nc.sync.dma_start(n3_sb[:], n3)
 
-        w_bf = sb.tile([P, PACK * N], BF16, name="w_bf", tag="w_bf", align_bytes=64)
+        w_bf = sb.tile([P, PACK * N], BF16, name="w_bf", tag="staging", align_bytes=64)
         w_dealt = w_bf[:].rearrange("p (t m j) -> p m t j", t=PACK, j=PACK)
         w_cols = w_raw[:].rearrange("p j (m t) -> p m t j", t=PACK)
         nc.scalar.copy(w_dealt[:, :M_SCALAR], w_cols[:, :M_SCALAR])
@@ -77,18 +81,18 @@ def tile_picked_nce8_none_po_kernel(
         w_scales = sb.tile([P, N], U8, name="w_scales", align_bytes=64)
         nc.vector.quantize_mx(out=w_codes[:].bitcast(FP8X4), scales=w_scales[:], in_=w_bf[:])
 
-        x_picked = sb.tile([P, S], U32, name="x_picked", tag="w_bf", align_bytes=64)
+        x_picked = sb.tile([P, S], U32, name="x_picked", tag="staging", align_bytes=64)
         for h in range(2):
             nc.vector.tensor_copy(x_picked[:, half(h)], x_table[:].indirect(entries(offs_sb, h)))
 
-        ident = sb.tile([P, P], F32, name="ident")
-        make_identity(nc, ident[:])
+        identity = sb.tile([P, P], F32, name="identity")
+        make_identity(nc, identity[:])
 
         def product(out, t, cols):
             nc.tensor.matmul_mx(
                 out=out,
-                lhsT=w_codes[:, t * P : (t + 1) * P].bitcast(FP8X4),
-                lhsT_scale=w_scales[:, t * P : (t + 1) * P],
+                lhsT=w_codes[:, block(t)].bitcast(FP8X4),
+                lhsT_scale=w_scales[:, block(t)],
                 rhs=x_picked[:, cols].bitcast(FP8X4),
                 rhs_scale=x_picked_scales[:, cols],
                 start=True,
@@ -97,133 +101,122 @@ def tile_picked_nce8_none_po_kernel(
 
         y_half = {}
         for h in range(2):
-            for t in range(2):
+            for t in (1, 0):
                 y_half[t, h] = ps.tile([P, HALF], F32, name="y_half%d%d" % (t, h), tag="bank%d%d" % (t, h))
                 product(y_half[t, h][:], t, half(h))
-        y_ps = {}
+        y_whole = {}
         for t in (2, 3):
-            y_ps[t] = ps.tile([P, S], F32, name="y_ps%d" % t)
-            product(y_ps[t][:], t, slice(0, S))
+            y_whole[t] = ps.tile([P, S], F32, name="y_whole%d" % t)
+            product(y_whole[t][:], t, slice(0, S))
 
-        exp_y = [sb.tile([P, 2 * S], F32, name="exp_y%d" % t) for t in range(PACK)]
-        y_sb = {t: sb.tile([P, 2 * S], F32, name="y_sb%d" % t) for t in (1, 3)}
-        own = {t: sb.tile([P, S], F32, name="own%d" % t) for t in (0, 2)}
-        neg = {(t, i): sb.tile([P, S], F32, name="neg%d%d" % (t, i)) for t in range(PACK) for i in range(3)}
         lists = (n1_sb, n2_sb, n3_sb)
-        sum_t = {t: ps.tile([P, S], F32, name="sum_t%d" % t) for t in (1, 3)}
-        log_sum = [sb.tile([P, S], F32, name="log_sum%d" % t) for t in range(PACK)]
+        exp_y = [sb.tile([P, width], F32, name="exp_y%d" % t) for t, width in enumerate((S, S, 2 * S, 2 * S))]
+        y_sb = {t: sb.tile([P, 2 * S], F32, name="y_sb%d" % t) for t in (0, 3)}
+        exp_neg_y = {t: sb.tile([P, S], F32, name="exp_neg_y%d" % t) for t in (1, 2)}
         loss = sb.tile([P, PACK, S], F32, name="loss")
+        ratio_2 = sb.tile([P, S], F32, name="ratio_2")
+        ratio = {1: loss[:, 2, :], 2: ratio_2[:]}
+        gathered = {(2, 0): ratio[1], (2, 2): exp_y[3][:, S:], (3, 2): loss[:, 1, :]}
+        for t in range(PACK):
+            for i in range(len(lists)):
+                if (t, i) not in gathered:
+                    own_bytes = sb.tile([P, S], F32, name="gathered%d%d" % (t, i))
+                    gathered[t, i] = own_bytes[:]
+        turned_sum = {t: ps.tile([P, S], F32, name="turned_sum%d" % t) for t in (0, 3)}
+        turned_log = {t: sb.tile([P, S], F32, name="turned_log%d" % t) for t in (0, 3)}
         loss_bf = [sb.tile([P, HALF * PACK], BF16, name="loss_bf%d" % h, align_bytes=64) for h in range(2)]
         out_codes = sb.tile([P, S], U32, name="out_codes", align_bytes=64)
         out_scales = sb.tile([P, S], U8, name="out_scales", align_bytes=64)
         out_rows = out_0.rearrange("(p t) j -> p t j", t=PACK)
         out_words = out_1[0].rearrange("p n j -> p (n j)").bitcast(I32)
 
-        ratio = sb.tile([P, 2, S], F32, name="ratio")
-        neg[2, 0] = log_sum[0] = ratio[:, 0, :]
-        neg[3, 2] = log_sum[2] = ratio[:, 1, :]
-        neg[2, 2] = exp_y[3][:, S:]
-
-        def block(b):
-            return slice(b * P, (b + 1) * P)
-
-        def scalar_negative(t, i):
-            nc.scalar.activation(neg[t, i][:], y_sb[t][:].indirect(lists[i][:]), ACT.Exp)
-
-        def add_negative(t, i, to):
-            nc.vector.tensor_tensor(neg[t, i][:], exp_y[t][:].indirect(lists[i][:]), to[:], ALU.add)
-
-        def add_transposed(t, term, first=False, last=False):
-            for b in range(PACK):
-                nc.tensor.matmul(
-                    sum_t[t][:, block(b)], term[:, block(b)], ident[:], is_transpose=True,
-                    start=first and b == 0, stop=last and b == PACK - 1,
-                )
-
-        def interleaved(h):
-            dst = loss_bf[h][:].rearrange("p (c i t) -> p c t i", i=4, t=PACK)
-            return dst, loss[:, :, half(h)].rearrange("p t (c i) -> p c t i", i=4)
-
-        def quantize_and_store(h):
-            nc.vector.quantize_mx(out=out_codes[:, half(h)].bitcast(FP8X4), scales=out_scales[:, half(h)], in_=loss_bf[h][:])
-
-        def first_negative(t, i):
-            nc.vector.tensor_copy(neg[t, i][:], exp_y[t][:].indirect(lists[i][:]))
-
-        def divide(t, cols):
-            nc.gpsimd.tensor_tensor(log_sum[t][:, cols], neg[t, 2][:, cols], own[t][:, cols], ALU.mult)
-
-        def log_and_store(t, parts):
-            for cols in parts:
-                nc.scalar.activation(loss[:, t, cols], log_sum[t][:, cols], ACT.Ln, bias=1.0)
-            nc.sync.dma_start(out_rows[:, t, :], loss[:, t, :])
-
-        def log_turn_back_and_store(t, banks):
-            for h in range(2):
-                nc.scalar.activation(log_sum[t][:, half(h)], sum_t[t][:, half(h)], ACT.Ln)
-                back = ps.tile([P, HALF], F32, name="back%d%d" % (t, h), tag=banks[h])
-                for b in range(2):
-                    nc.tensor.transpose(back[:, block(b)], log_sum[t][:, block(2 * h + b)], ident[:])
-                nc.vector.tensor_tensor(loss[:, t, half(h)], back[:], y_sb[t][:, half(h)], ALU.subtract)
-            nc.sync.dma_start(out_rows[:, t, :], loss[:, t, :])
+        def scalar_gather(t, i):
+            nc.scalar.activation(gathered[t, i], y_sb[t][:].indirect(lists[i][:]), ACT.Exp)
 
         def chain(t, i):
             for h in range(2):
                 looked_up = exp_y[t][:].indirect(entries(lists[i], h))
                 if i == 0:
-                    nc.vector.tensor_copy(neg[t, i][:, half(h)], looked_up)
+                    nc.vector.tensor_copy(gathered[t, i][:, half(h)], looked_up)
                 else:
-                    nc.vector.tensor_tensor(neg[t, i][:, half(h)], looked_up, neg[t, i - 1][:, half(h)], ALU.add)
+                    nc.vector.tensor_tensor(
+                        gathered[t, i][:, half(h)], looked_up, gathered[t, i - 1][:, half(h)], ALU.add
+                    )
 
-        whole = slice(0, S)
-        nc.vector.tensor_copy(y_sb[1][:, half(0)], y_half[1, 0][:])
+        def add_turned(t, term, first=False, last=False):
+            for b in range(BLOCKS):
+                nc.tensor.matmul(
+                    turned_sum[t][:, block(b)],
+                    term[:, block(b)],
+                    identity[:],
+                    is_transpose=True,
+                    start=first and b == 0,
+                    stop=last and b == BLOCKS - 1,
+                )
+
+        def log_and_turn_back(t, free_banks):
+            for h in range(2):
+                nc.scalar.activation(turned_log[t][:, half(h)], turned_sum[t][:, half(h)], ACT.Ln)
+                log_sum = ps.tile([P, HALF], F32, name="log_sum%d%d" % (t, h), tag=free_banks[h])
+                for b in range(BLOCKS // 2):
+                    nc.tensor.transpose(log_sum[:, block(b)], turned_log[t][:, block(2 * h + b)], identity[:])
+                nc.vector.tensor_tensor(loss[:, t, half(h)], log_sum[:], y_sb[t][:, half(h)], ALU.subtract)
+
+        def interleaved(h):
+            dst = loss_bf[h][:].rearrange("p (c i t) -> p c t i", i=4, t=PACK)
+            return dst, loss[:, :, half(h)].rearrange("p t (c i) -> p c t i", i=4)
+
+        nc.vector.tensor_copy(y_sb[0][:, half(0)], y_half[0, 0][:])
         for h in range(2):
-            nc.scalar.activation(exp_y[0][:, half(h)], y_half[0, h][:], ACT.Exp)
-        nc.vector.tensor_copy(y_sb[1][:, half(1)], y_half[1, 1][:])
-        nc.scalar.activation(exp_y[2][:, :S], y_ps[2][:], ACT.Exp)
+            nc.scalar.activation(exp_y[1][:, half(h)], y_half[1, h][:], ACT.Exp)
+        nc.vector.tensor_copy(y_sb[0][:, half(1)], y_half[0, 1][:])
+        nc.scalar.activation(exp_y[2][:, :S], y_whole[2][:], ACT.Exp)
         for i in range(3):
-            chain(0, i)
-        scalar_negative(1, 0)
-        add_transposed(1, neg[1, 0], first=True)
-        nc.scalar.activation(exp_y[3][:, :S], y_ps[3][:], ACT.Exp)
-        add_transposed(3, exp_y[3], first=True)
-        nc.scalar.copy(y_sb[3][:, :S], y_ps[3][:])
+            chain(1, i)
+        scalar_gather(0, 0)
+        add_turned(0, gathered[0, 0], first=True)
+        nc.scalar.activation(exp_y[3][:, :S], y_whole[3][:], ACT.Exp)
+        add_turned(3, exp_y[3], first=True)
+        nc.scalar.copy(y_sb[3][:, :S], y_whole[3][:])
         for h in range(2):
-            nc.scalar.activation(own[0][:, half(h)], y_half[0, h][:], ACT.Exp, scale=-1.0)
+            nc.scalar.activation(exp_neg_y[1][:, half(h)], y_half[1, h][:], ACT.Exp, scale=-1.0)
         for i in range(2):
             chain(2, i)
-        divide(0, whole)
-        first_negative(3, 1)
-        first_negative(3, 2)
-        add_negative(2, 2, neg[2, 1])
-        scalar_negative(1, 1)
-        add_transposed(1, neg[1, 1])
-        scalar_negative(1, 2)
-        add_transposed(1, neg[1, 2])
-        nc.scalar.activation(exp_y[1][:, :S], y_sb[1][:, :S], ACT.Exp)
-        add_transposed(1, exp_y[1], last=True)
-        scalar_negative(3, 0)
-        add_transposed(3, neg[3, 0])
-        add_transposed(3, neg[3, 1])
-        add_transposed(3, neg[3, 2], last=True)
-        nc.scalar.activation(own[2][:], y_ps[2][:], ACT.Exp, scale=-1.0)
+        nc.gpsimd.tensor_tensor(ratio[1], gathered[1, 2], exp_neg_y[1][:], ALU.mult)
+        for i in (1, 2):
+            nc.vector.tensor_copy(gathered[3, i], exp_y[3][:].indirect(lists[i][:]))
+        nc.vector.tensor_tensor(gathered[2, 2], exp_y[2][:].indirect(n3_sb[:]), gathered[2, 1], ALU.add)
+        for i in (1, 2):
+            scalar_gather(0, i)
+            add_turned(0, gathered[0, i])
+        nc.scalar.activation(exp_y[0][:], y_sb[0][:, :S], ACT.Exp)
+        add_turned(0, exp_y[0], last=True)
+        scalar_gather(3, 0)
+        for i in range(3):
+            add_turned(3, gathered[3, i], last=i == 2)
+        nc.scalar.activation(exp_neg_y[2][:], y_whole[2][:], ACT.Exp, scale=-1.0)
         for h in range(2):
-            divide(2, half(h))
+            nc.gpsimd.tensor_tensor(ratio[2][:, half(h)], gathered[2, 2][:, half(h)], exp_neg_y[2][:, half(h)], ALU.mult)
 
-        log_turn_back_and_store(1, ("bank00", "bank01"))
-        log_turn_back_and_store(3, ("bank10", "bank11"))
+        log_and_turn_back(0, ("bank10", "bank11"))
+        nc.sync.dma_start(out_rows[:, 0, :], loss[:, 0, :])
+        log_and_turn_back(3, ("bank00", "bank01"))
+        nc.scalar.activation(loss[:, 1, :], ratio[1], ACT.Ln, bias=1.0)
+        nc.sync.dma_start(out_rows[:, 1, :], loss[:, 1, :])
         for h in range(2):
-            nc.scalar.activation(loss[:, 0:PACK:2, half(h)], ratio[:, :, half(h)], ACT.Ln, bias=1.0)
-            nc.sync.dma_start(out_rows[:, 0:PACK:2, half(h)], loss[:, 0:PACK:2, half(h)])
+            nc.scalar.activation(loss[:, 2, half(h)], ratio[2][:, half(h)], ACT.Ln, bias=1.0)
+        nc.sync.dma_start(out_rows[:, 2:, :], loss[:, 2:, :])
 
         dst, src = interleaved(0)
         nc.vector.tensor_copy(dst, src)
         dst, src = interleaved(1)
         nc.scalar.copy(dst[:, : J_SCALAR // 4], src[:, : J_SCALAR // 4])
         nc.vector.tensor_copy(dst[:, J_SCALAR // 4 :], src[:, J_SCALAR // 4 :])
-        quantize_and_store(0)
-        quantize_and_store(1)
-        nc.sync.dma_start(out_words, out_codes[:].bitcast(I32))
+        for h in range(2):
+            nc.vector.quantize_mx(
+                out=out_codes[:, half(h)].bitcast(FP8X4), scales=out_scales[:, half(h)], in_=loss_bf[h][:]
+            )
+            nc.sync.dma_start(out_words[:, half(h)], out_codes[:, half(h)].bitcast(I32))
         for q in range(QUADRANTS):
             partitions, rows = scale_rows(q)
             queue = nc.scalar if q % 2 else nc.sync

@@ -22,7 +22,7 @@ QUADRANTS = 4
 HALF = S // 2
 LIST_COLS = HALF // 16
 BLOCKS = S // P
-M_SCALAR = 48
+M_SCALAR = 80
 J_SCALAR = 128
 
 
@@ -61,13 +61,12 @@ def tile_picked_nce8_none_po_kernel(
         nc.vector.memset(xs_table[:, : T // 2].bitcast(I32), 0)
         nc.gpsimd.memset(xs_table[:, T // 2 :].bitcast(I32), 0)
         nc.sync.dma_start(offs_sb[:], offs)
+        nc.sync.dma_start(w_raw[:], w1.rearrange("(p j) c -> p j c", j=PACK))
+        for r in range(4):
+            nc.sync.dma_start(xs_table[r:P:32, :].bitcast(I32), x_scales[0, r:16:4, :].bitcast(I32))
+        nc.sync.dma_start(x_table[:].bitcast(I32), x_words[0].rearrange("p n j -> p (n j)").bitcast(I32))
         nc.sync.dma_start(n1_sb[:], n1)
         nc.sync.dma_start(n2_sb[:], n2)
-        nc.sync.dma_start(w_raw[:], w1.rearrange("(p j) c -> p j c", j=PACK))
-        for q in range(QUADRANTS):
-            partitions, rows = scale_rows(q)
-            nc.sync.dma_start(xs_table[partitions, :].bitcast(I32), x_scales[0, rows, :].bitcast(I32))
-        nc.sync.dma_start(x_table[:].bitcast(I32), x_words[0].rearrange("p n j -> p (n j)").bitcast(I32))
         nc.sync.dma_start(n3_sb[:], n3)
 
         w_bf = sb.tile([P, PACK * N], BF16, name="w_bf", tag="staging", align_bytes=64)
@@ -101,28 +100,28 @@ def tile_picked_nce8_none_po_kernel(
 
         y_half = {}
         for h in range(2):
-            for t in (1, 0):
+            for t in (1, 0, 2):
                 y_half[t, h] = ps.tile([P, HALF], F32, name="y_half%d%d" % (t, h), tag="bank%d%d" % (t, h))
                 product(y_half[t, h][:], t, half(h))
         y_whole = {}
-        for t in (2, 3):
+        for t in (3,):
             y_whole[t] = ps.tile([P, S], F32, name="y_whole%d" % t)
             product(y_whole[t][:], t, slice(0, S))
 
         lists = (n1_sb, n2_sb, n3_sb)
-        exp_y = [sb.tile([P, width], F32, name="exp_y%d" % t) for t, width in enumerate((S, S, 2 * S, 2 * S))]
+        exp_y = [sb.tile([P, width], F32, name="exp_y%d" % t) for t, width in enumerate((S, 2 * S, 2 * S, 2 * S))]
         y_sb = {t: sb.tile([P, 2 * S], F32, name="y_sb%d" % t) for t in (0, 3)}
         exp_neg_y = {t: sb.tile([P, S], F32, name="exp_neg_y%d" % t) for t in (1, 2)}
         loss = sb.tile([P, PACK, S], F32, name="loss")
         ratio_2 = sb.tile([P, S], F32, name="ratio_2")
         ratio = {1: loss[:, 2, :], 2: ratio_2[:]}
-        gathered = {(2, 0): ratio[1], (2, 2): exp_y[3][:, S:], (3, 2): loss[:, 1, :]}
+        gathered = {(2, 2): exp_y[3][:, S:], (3, 2): loss[:, 1, :]}
         for t in range(PACK):
             for i in range(len(lists)):
                 if (t, i) not in gathered:
                     own_bytes = sb.tile([P, S], F32, name="gathered%d%d" % (t, i))
                     gathered[t, i] = own_bytes[:]
-        turned_sum = {t: ps.tile([P, S], F32, name="turned_sum%d" % t) for t in (0, 3)}
+        turned_sum = {}
         turned_log = {t: sb.tile([P, S], F32, name="turned_log%d" % t) for t in (0, 3)}
         loss_bf = [sb.tile([P, HALF * PACK], BF16, name="loss_bf%d" % h, align_bytes=64) for h in range(2)]
         out_codes = sb.tile([P, S], U32, name="out_codes", align_bytes=64)
@@ -134,16 +133,15 @@ def tile_picked_nce8_none_po_kernel(
             nc.scalar.activation(gathered[t, i], y_sb[t][:].indirect(lists[i][:]), ACT.Exp)
 
         def chain(t, i):
-            for h in range(2):
-                looked_up = exp_y[t][:].indirect(entries(lists[i], h))
-                if i == 0:
-                    nc.vector.tensor_copy(gathered[t, i][:, half(h)], looked_up)
-                else:
-                    nc.vector.tensor_tensor(
-                        gathered[t, i][:, half(h)], looked_up, gathered[t, i - 1][:, half(h)], ALU.add
-                    )
+            looked_up = exp_y[t][:].indirect(lists[i][:])
+            if i == 0:
+                nc.vector.tensor_copy(gathered[t, i], looked_up)
+            else:
+                nc.vector.tensor_tensor(gathered[t, i], looked_up, gathered[t, i - 1], ALU.add)
 
         def add_turned(t, term, first=False, last=False):
+            if first:
+                turned_sum[t] = ps.tile([P, S], F32, name="turned_sum%d" % t, tag="bank00" if t == 3 else "bank_free")
             for b in range(BLOCKS):
                 nc.tensor.matmul(
                     turned_sum[t][:, block(b)],
@@ -166,13 +164,14 @@ def tile_picked_nce8_none_po_kernel(
             dst = loss_bf[h][:].rearrange("p (c i t) -> p c t i", i=4, t=PACK)
             return dst, loss[:, :, half(h)].rearrange("p t (c i) -> p c t i", i=4)
 
-        nc.vector.tensor_copy(y_sb[0][:, half(0)], y_half[0, 0][:])
         for h in range(2):
-            nc.scalar.activation(exp_y[1][:, half(h)], y_half[1, h][:], ACT.Exp)
-        nc.vector.tensor_copy(y_sb[0][:, half(1)], y_half[0, 1][:])
-        nc.scalar.activation(exp_y[2][:, :S], y_whole[2][:], ACT.Exp)
-        for i in range(3):
-            chain(1, i)
+            nc.vector.tensor_copy(y_sb[0][:, half(h)], y_half[0, h][:])
+            for t in (1, 2):
+                nc.scalar.activation(exp_y[t][:, half(h)], y_half[t, h][:], ACT.Exp)
+        for i in range(2):
+            for t in (1, 2):
+                chain(t, i)
+        chain(1, 2)
         scalar_gather(0, 0)
         add_turned(0, gathered[0, 0], first=True)
         nc.scalar.activation(exp_y[3][:, :S], y_whole[3][:], ACT.Exp)
@@ -180,8 +179,6 @@ def tile_picked_nce8_none_po_kernel(
         nc.scalar.copy(y_sb[3][:, :S], y_whole[3][:])
         for h in range(2):
             nc.scalar.activation(exp_neg_y[1][:, half(h)], y_half[1, h][:], ACT.Exp, scale=-1.0)
-        for i in range(2):
-            chain(2, i)
         nc.gpsimd.tensor_tensor(ratio[1], gathered[1, 2], exp_neg_y[1][:], ALU.mult)
         for i in (1, 2):
             nc.vector.tensor_copy(gathered[3, i], exp_y[3][:].indirect(lists[i][:]))
@@ -194,13 +191,14 @@ def tile_picked_nce8_none_po_kernel(
         scalar_gather(3, 0)
         for i in range(3):
             add_turned(3, gathered[3, i], last=i == 2)
-        nc.scalar.activation(exp_neg_y[2][:], y_whole[2][:], ACT.Exp, scale=-1.0)
+        for h in range(2):
+            nc.scalar.activation(exp_neg_y[2][:, half(h)], y_half[2, h][:], ACT.Exp, scale=-1.0)
         for h in range(2):
             nc.gpsimd.tensor_tensor(ratio[2][:, half(h)], gathered[2, 2][:, half(h)], exp_neg_y[2][:, half(h)], ALU.mult)
 
         log_and_turn_back(0, ("bank10", "bank11"))
         nc.sync.dma_start(out_rows[:, 0, :], loss[:, 0, :])
-        log_and_turn_back(3, ("bank00", "bank01"))
+        log_and_turn_back(3, ("bank20", "bank21"))
         nc.scalar.activation(loss[:, 1, :], ratio[1], ACT.Ln, bias=1.0)
         nc.sync.dma_start(out_rows[:, 1, :], loss[:, 1, :])
         for h in range(2):

@@ -22,7 +22,7 @@ QUADRANTS = 4
 HALF = S // 2
 LIST_COLS = HALF // 16
 BLOCKS = S // P
-M_SCALAR = 80
+M_SCALAR = 24
 J_SCALAR = 128
 
 
@@ -54,16 +54,18 @@ def tile_picked_nce8_none_po_kernel(
         n1_sb = sb.tile([P, S // 16], U16, name="n1_sb")
         n2_sb = sb.tile([P, S // 16], U16, name="n2_sb")
         n3_sb = sb.tile([P, S // 16], U16, name="n3_sb")
-        w_raw = sb.tile([P, PACK, N], F32, name="w_raw")
+        w_raw = [sb.tile([P, PACK, N // 2], F32, name="w_raw%d" % h) for h in range(2)]
+        w_rows = w1.rearrange("(p j) c -> p j c", j=PACK)
         x_table = sb.tile([P, T], U32, name="x_table")
         xs_table = sb.tile([P, T], U8, name="xs_table")
 
         nc.vector.memset(xs_table[:, : T // 2].bitcast(I32), 0)
         nc.gpsimd.memset(xs_table[:, T // 2 :].bitcast(I32), 0)
         nc.sync.dma_start(offs_sb[:], offs)
-        nc.sync.dma_start(w_raw[:], w1.rearrange("(p j) c -> p j c", j=PACK))
+        nc.sync.dma_start(w_raw[0][:], w_rows[:, :, half(0)])
         for r in range(4):
             nc.sync.dma_start(xs_table[r:P:32, :].bitcast(I32), x_scales[0, r:16:4, :].bitcast(I32))
+        nc.sync.dma_start(w_raw[1][:], w_rows[:, :, half(1)])
         nc.sync.dma_start(x_table[:].bitcast(I32), x_words[0].rearrange("p n j -> p (n j)").bitcast(I32))
         nc.sync.dma_start(n1_sb[:], n1)
         nc.sync.dma_start(n2_sb[:], n2)
@@ -71,9 +73,11 @@ def tile_picked_nce8_none_po_kernel(
 
         w_bf = sb.tile([P, PACK * N], BF16, name="w_bf", tag="staging", align_bytes=64)
         w_dealt = w_bf[:].rearrange("p (t m j) -> p m t j", t=PACK, j=PACK)
-        w_cols = w_raw[:].rearrange("p j (m t) -> p m t j", t=PACK)
-        nc.scalar.copy(w_dealt[:, :M_SCALAR], w_cols[:, :M_SCALAR])
-        nc.vector.tensor_copy(w_dealt[:, M_SCALAR:], w_cols[:, M_SCALAR:])
+        for h in range(2):
+            w_cols = w_raw[h][:].rearrange("p j (m t) -> p m t j", t=PACK)
+            m0 = h * P // 2
+            nc.scalar.copy(w_dealt[:, m0 : m0 + M_SCALAR], w_cols[:, :M_SCALAR])
+            nc.vector.tensor_copy(w_dealt[:, m0 + M_SCALAR : m0 + P // 2], w_cols[:, M_SCALAR:])
         x_picked_scales = sb.tile([P, S], U8, name="x_picked_scales", align_bytes=64)
         nc.vector.tensor_copy(x_picked_scales[:], xs_table[:].indirect(offs_sb[:]))
         w_codes = sb.tile([P, N], U32, name="w_codes", align_bytes=64)

@@ -23,7 +23,7 @@ HALF = S // 2
 LIST_COLS = HALF // 16
 BLOCKS = S // P
 M_SCALAR = 24
-J_SCALAR = 128
+J_SCALAR = 192
 
 
 def half(h):
@@ -119,7 +119,8 @@ def tile_picked_nce8_none_po_kernel(
         loss = sb.tile([P, PACK, S], F32, name="loss")
         ratio_2 = sb.tile([P, S], F32, name="ratio_2")
         ratio = {1: loss[:, 2, :], 2: ratio_2[:]}
-        gathered = {(2, 2): exp_y[3][:, S:], (3, 2): loss[:, 1, :]}
+        last_link = sb.tile([P, S], F32, name="last_link")
+        gathered = {(1, 2): last_link[:], (2, 2): last_link[:], (3, 2): loss[:, 1, :]}
         for t in range(PACK):
             for i in range(len(lists)):
                 if (t, i) not in gathered:
@@ -186,7 +187,9 @@ def tile_picked_nce8_none_po_kernel(
         nc.gpsimd.tensor_tensor(ratio[1], gathered[1, 2], exp_neg_y[1][:], ALU.mult)
         for i in (1, 2):
             nc.vector.tensor_copy(gathered[3, i], exp_y[3][:].indirect(lists[i][:]))
-        nc.vector.tensor_tensor(gathered[2, 2], exp_y[2][:].indirect(n3_sb[:]), gathered[2, 1], ALU.add)
+        for h in range(2):
+            looked_up = exp_y[2][:].indirect(entries(n3_sb, h))
+            nc.vector.tensor_tensor(gathered[2, 2][:, half(h)], looked_up, gathered[2, 1][:, half(h)], ALU.add)
         for i in (1, 2):
             scalar_gather(0, i)
             add_turned(0, gathered[0, i])
@@ -198,13 +201,12 @@ def tile_picked_nce8_none_po_kernel(
         for h in range(2):
             nc.scalar.activation(exp_neg_y[2][:, half(h)], y_half[2, h][:], ACT.Exp, scale=-1.0)
         for h in range(2):
-            nc.gpsimd.tensor_tensor(ratio[2][:, half(h)], gathered[2, 2][:, half(h)], exp_neg_y[2][:, half(h)], ALU.mult)
+            nc.vector.tensor_tensor(ratio[2][:, half(h)], gathered[2, 2][:, half(h)], exp_neg_y[2][:, half(h)], ALU.mult)
 
         log_and_turn_back(0, ("bank10", "bank11"))
-        nc.sync.dma_start(out_rows[:, 0, :], loss[:, 0, :])
         log_and_turn_back(3, ("bank20", "bank21"))
         nc.scalar.activation(loss[:, 1, :], ratio[1], ACT.Ln, bias=1.0)
-        nc.sync.dma_start(out_rows[:, 1, :], loss[:, 1, :])
+        nc.sync.dma_start(out_rows[:, :2, :], loss[:, :2, :])
         for h in range(2):
             nc.scalar.activation(loss[:, 2, half(h)], ratio[2][:, half(h)], ACT.Ln, bias=1.0)
         nc.sync.dma_start(out_rows[:, 2:, :], loss[:, 2:, :])

@@ -22,8 +22,8 @@ QUADRANTS = 4
 HALF = S // 2
 LIST_COLS = HALF // 16
 BLOCKS = S // P
-M_SCALAR = 24
-J_SCALAR = 192
+M_SCALAR = 28
+J_SCALAR = 128
 
 
 def half(h):
@@ -103,10 +103,9 @@ def tile_picked_nce8_none_po_kernel(
             )
 
         y_half = {}
-        for h in range(2):
-            for t in (1, 0, 2):
-                y_half[t, h] = ps.tile([P, HALF], F32, name="y_half%d%d" % (t, h), tag="bank%d%d" % (t, h))
-                product(y_half[t, h][:], t, half(h))
+        for t, h in ((1, 0), (0, 0), (1, 1), (0, 1), (2, 0), (2, 1)):
+            y_half[t, h] = ps.tile([P, HALF], F32, name="y_half%d%d" % (t, h), tag="bank%d%d" % (t, h))
+            product(y_half[t, h][:], t, half(h))
         y_whole = {}
         for t in (3,):
             y_whole[t] = ps.tile([P, S], F32, name="y_whole%d" % t)
@@ -136,6 +135,9 @@ def tile_picked_nce8_none_po_kernel(
 
         def scalar_gather(t, i):
             nc.scalar.activation(gathered[t, i], y_sb[t][:].indirect(lists[i][:]), ACT.Exp)
+
+        def exp_neg(t, h):
+            nc.scalar.activation(exp_neg_y[t][:, half(h)], y_half[t, h][:], ACT.Exp, scale=-1.0)
 
         def chain(t, i):
             looked_up = exp_y[t][:].indirect(lists[i][:])
@@ -171,19 +173,22 @@ def tile_picked_nce8_none_po_kernel(
 
         for h in range(2):
             nc.vector.tensor_copy(y_sb[0][:, half(h)], y_half[0, h][:])
-            for t in (1, 2):
-                nc.scalar.activation(exp_y[t][:, half(h)], y_half[t, h][:], ACT.Exp)
-        for i in range(2):
-            for t in (1, 2):
-                chain(t, i)
-        chain(1, 2)
+            nc.scalar.activation(exp_y[1][:, half(h)], y_half[1, h][:], ACT.Exp)
+            exp_neg(1, h)
+        for h in range(2):
+            nc.scalar.activation(exp_y[2][:, half(h)], y_half[2, h][:], ACT.Exp)
+        for h in range(2):
+            nc.vector.tensor_copy(gathered[1, 0][:, half(h)], exp_y[1][:].indirect(entries(n1_sb, h)))
+        for h in range(2):
+            looked_up = exp_y[1][:].indirect(entries(n2_sb, h))
+            nc.vector.tensor_tensor(gathered[1, 1][:, half(h)], looked_up, gathered[1, 0][:, half(h)], ALU.add)
+        for t, i in ((2, 0), (1, 2), (2, 1)):
+            chain(t, i)
         scalar_gather(0, 0)
-        add_turned(0, gathered[0, 0], first=True)
         nc.scalar.activation(exp_y[3][:, :S], y_whole[3][:], ACT.Exp)
+        add_turned(0, gathered[0, 0], first=True)
         add_turned(3, exp_y[3], first=True)
         nc.scalar.copy(y_sb[3][:, :S], y_whole[3][:])
-        for h in range(2):
-            nc.scalar.activation(exp_neg_y[1][:, half(h)], y_half[1, h][:], ACT.Exp, scale=-1.0)
         nc.gpsimd.tensor_tensor(ratio[1], gathered[1, 2], exp_neg_y[1][:], ALU.mult)
         for i in (1, 2):
             nc.vector.tensor_copy(gathered[3, i], exp_y[3][:].indirect(lists[i][:]))
@@ -199,14 +204,15 @@ def tile_picked_nce8_none_po_kernel(
         for i in range(3):
             add_turned(3, gathered[3, i], last=i == 2)
         for h in range(2):
-            nc.scalar.activation(exp_neg_y[2][:, half(h)], y_half[2, h][:], ACT.Exp, scale=-1.0)
+            exp_neg(2, h)
         for h in range(2):
-            nc.vector.tensor_tensor(ratio[2][:, half(h)], gathered[2, 2][:, half(h)], exp_neg_y[2][:, half(h)], ALU.mult)
+            nc.gpsimd.tensor_tensor(ratio[2][:, half(h)], gathered[2, 2][:, half(h)], exp_neg_y[2][:, half(h)], ALU.mult)
 
         log_and_turn_back(0, ("bank10", "bank11"))
+        nc.sync.dma_start(out_rows[:, 0, :], loss[:, 0, :])
         log_and_turn_back(3, ("bank20", "bank21"))
         nc.scalar.activation(loss[:, 1, :], ratio[1], ACT.Ln, bias=1.0)
-        nc.sync.dma_start(out_rows[:, :2, :], loss[:, :2, :])
+        nc.sync.dma_start(out_rows[:, 1, :], loss[:, 1, :])
         for h in range(2):
             nc.scalar.activation(loss[:, 2, half(h)], ratio[2][:, half(h)], ACT.Ln, bias=1.0)
         nc.sync.dma_start(out_rows[:, 2:, :], loss[:, 2:, :])

@@ -23,7 +23,7 @@ HALF = S // 2
 LIST_COLS = HALF // 16
 BLOCKS = S // P
 M_SCALAR = 28
-J_SCALAR = 128
+J_SCALAR = 96
 
 
 def half(h):
@@ -61,8 +61,8 @@ def tile_picked_nce8_none_po_kernel(
 
         nc.vector.memset(xs_table[:, : T // 2].bitcast(I32), 0)
         nc.gpsimd.memset(xs_table[:, T // 2 :].bitcast(I32), 0)
-        nc.sync.dma_start(offs_sb[:], offs)
         nc.sync.dma_start(w_raw[0][:], w_rows[:, :, half(0)])
+        nc.sync.dma_start(offs_sb[:], offs)
         for r in range(4):
             nc.sync.dma_start(xs_table[r:P:32, :].bitcast(I32), x_scales[0, r:16:4, :].bitcast(I32))
         nc.sync.dma_start(w_raw[1][:], w_rows[:, :, half(1)])

@@ -22,7 +22,7 @@ QUADRANTS = 4
 HALF = S // 2
 LIST_COLS = HALF // 16
 BLOCKS = S // P
-M_SCALAR = 28
+M_SCALAR = 48
 J_SCALAR = 96
 
 
@@ -54,18 +54,18 @@ def tile_picked_nce8_none_po_kernel(
         n1_sb = sb.tile([P, S // 16], U16, name="n1_sb")
         n2_sb = sb.tile([P, S // 16], U16, name="n2_sb")
         n3_sb = sb.tile([P, S // 16], U16, name="n3_sb")
-        w_raw = [sb.tile([P, PACK, N // 2], F32, name="w_raw%d" % h) for h in range(2)]
+        w_raw = sb.tile([P, PACK, N], F32, name="w_raw")
         w_rows = w1.rearrange("(p j) c -> p j c", j=PACK)
         x_table = sb.tile([P, T], U32, name="x_table")
         xs_table = sb.tile([P, T], U8, name="xs_table")
 
         nc.vector.memset(xs_table[:, : T // 2].bitcast(I32), 0)
         nc.gpsimd.memset(xs_table[:, T // 2 :].bitcast(I32), 0)
-        nc.sync.dma_start(w_raw[0][:], w_rows[:, :, half(0)])
+        nc.sync.dma_start(w_raw[:, :2, :], w_rows[:, :2, :])
         nc.sync.dma_start(offs_sb[:], offs)
         for r in range(4):
             nc.sync.dma_start(xs_table[r:P:32, :].bitcast(I32), x_scales[0, r:16:4, :].bitcast(I32))
-        nc.sync.dma_start(w_raw[1][:], w_rows[:, :, half(1)])
+        nc.sync.dma_start(w_raw[:, 2:, :], w_rows[:, 2:, :])
         nc.sync.dma_start(x_table[:].bitcast(I32), x_words[0].rearrange("p n j -> p (n j)").bitcast(I32))
         nc.sync.dma_start(n1_sb[:], n1)
         nc.sync.dma_start(n2_sb[:], n2)
@@ -73,13 +73,12 @@ def tile_picked_nce8_none_po_kernel(
 
         w_bf = sb.tile([P, PACK * N], BF16, name="w_bf", tag="staging", align_bytes=64)
         w_dealt = w_bf[:].rearrange("p (t m j) -> p m t j", t=PACK, j=PACK)
-        for h in range(2):
-            w_cols = w_raw[h][:].rearrange("p j (m t) -> p m t j", t=PACK)
-            m0 = h * P // 2
-            nc.scalar.copy(w_dealt[:, m0 : m0 + M_SCALAR], w_cols[:, :M_SCALAR])
-            nc.vector.tensor_copy(w_dealt[:, m0 + M_SCALAR : m0 + P // 2], w_cols[:, M_SCALAR:])
         x_picked_scales = sb.tile([P, S], U8, name="x_picked_scales", align_bytes=64)
         nc.vector.tensor_copy(x_picked_scales[:], xs_table[:].indirect(offs_sb[:]))
+        w_cols = w_raw[:].rearrange("p j (m t) -> p m t j", t=PACK)
+        for pair in (slice(0, 2), slice(2, 4)):
+            nc.scalar.copy(w_dealt[:, :M_SCALAR, :, pair], w_cols[:, :M_SCALAR, :, pair])
+        nc.vector.tensor_copy(w_dealt[:, M_SCALAR:], w_cols[:, M_SCALAR:])
         w_codes = sb.tile([P, N], U32, name="w_codes", align_bytes=64)
         w_scales = sb.tile([P, N], U8, name="w_scales", align_bytes=64)
         nc.vector.quantize_mx(out=w_codes[:].bitcast(FP8X4), scales=w_scales[:], in_=w_bf[:])

@@ -84,8 +84,8 @@ def tile_picked_nce8_none_po_kernel(
         nc.vector.quantize_mx(out=w_codes[:].bitcast(FP8X4), scales=w_scales[:], in_=w_bf[:])
 
         x_picked = sb.tile([P, S], U32, name="x_picked", tag="staging", align_bytes=64)
-        for h in range(2):
-            nc.vector.tensor_copy(x_picked[:, half(h)], x_table[:].indirect(entries(offs_sb, h)))
+        for cols in (block(0), block(1), half(1)):
+            nc.vector.tensor_copy(x_picked[:, cols], x_table[:].indirect(offs_sb[:, cols.start // 16 : cols.stop // 16]))
 
         identity = sb.tile([P, P], F32, name="identity")
         make_identity(nc, identity[:])
@@ -101,14 +101,18 @@ def tile_picked_nce8_none_po_kernel(
                 stop=True,
             )
 
+        y_1 = [ps.tile([P, P], F32, name="y_1%d" % b, tag="bank_a%d" % b) for b in range(2)]
         y_half = {}
-        for t, h in ((1, 0), (0, 0), (1, 1), (0, 1), (2, 0), (2, 1)):
+        for t, h in ((0, 0), (3, 0), (1, 1), (0, 1), (3, 1)):
             y_half[t, h] = ps.tile([P, HALF], F32, name="y_half%d%d" % (t, h), tag="bank%d%d" % (t, h))
+        y_2 = ps.tile([P, S], F32, name="y_2")
+        for b in range(2):
+            product(y_1[b][:], 1, block(b))
+            product(y_half[0, 0][:, block(b)], 0, block(b))
+        for t, h in ((3, 0), (1, 1), (0, 1)):
             product(y_half[t, h][:], t, half(h))
-        y_whole = {}
-        for t in (3,):
-            y_whole[t] = ps.tile([P, S], F32, name="y_whole%d" % t)
-            product(y_whole[t][:], t, slice(0, S))
+        product(y_2[:], 2, slice(0, S))
+        product(y_half[3, 1][:], 3, half(1))
 
         lists = (n1_sb, n2_sb, n3_sb)
         exp_y = [sb.tile([P, width], F32, name="exp_y%d" % t) for t, width in enumerate((S, 2 * S, 2 * S, 2 * S))]
@@ -135,8 +139,8 @@ def tile_picked_nce8_none_po_kernel(
         def scalar_gather(t, i):
             nc.scalar.activation(gathered[t, i], y_sb[t][:].indirect(lists[i][:]), ACT.Exp)
 
-        def exp_neg(t, h):
-            nc.scalar.activation(exp_neg_y[t][:, half(h)], y_half[t, h][:], ACT.Exp, scale=-1.0)
+        def exp_neg(t, cols, y):
+            nc.scalar.activation(exp_neg_y[t][:, cols], y, ACT.Exp, scale=-1.0)
 
         def chain(t, i):
             looked_up = exp_y[t][:].indirect(lists[i][:])
@@ -147,7 +151,7 @@ def tile_picked_nce8_none_po_kernel(
 
         def add_turned(t, term, first=False, last=False):
             if first:
-                turned_sum[t] = ps.tile([P, S], F32, name="turned_sum%d" % t, tag="bank00" if t == 3 else "bank_free")
+                turned_sum[t] = ps.tile([P, S], F32, name="turned_sum%d" % t, tag="bank_a%d" % (t // 3))
             for b in range(BLOCKS):
                 nc.tensor.matmul(
                     turned_sum[t][:, block(b)],
@@ -170,12 +174,16 @@ def tile_picked_nce8_none_po_kernel(
             dst = loss_bf[h][:].rearrange("p (c i t) -> p c t i", i=4, t=PACK)
             return dst, loss[:, :, half(h)].rearrange("p t (c i) -> p c t i", i=4)
 
-        for h in range(2):
-            nc.vector.tensor_copy(y_sb[0][:, half(h)], y_half[0, h][:])
-            nc.scalar.activation(exp_y[1][:, half(h)], y_half[1, h][:], ACT.Exp)
-            exp_neg(1, h)
-        for h in range(2):
-            nc.scalar.activation(exp_y[2][:, half(h)], y_half[2, h][:], ACT.Exp)
+        for b in range(2):
+            nc.scalar.activation(exp_y[1][:, block(b)], y_1[b][:], ACT.Exp)
+            exp_neg(1, block(b), y_1[b][:])
+        nc.vector.tensor_copy(y_sb[0][:, half(0)], y_half[0, 0][:])
+        nc.scalar.activation(exp_y[3][:, half(0)], y_half[3, 0][:], ACT.Exp)
+        nc.vector.tensor_copy(y_sb[3][:, half(0)], y_half[3, 0][:])
+        nc.scalar.activation(exp_y[1][:, half(1)], y_half[1, 1][:], ACT.Exp)
+        exp_neg(1, half(1), y_half[1, 1][:])
+        nc.scalar.copy(y_sb[0][:, half(1)], y_half[0, 1][:])
+        nc.scalar.activation(exp_y[2][:, :S], y_2[:], ACT.Exp)
         for h in range(2):
             nc.vector.tensor_copy(gathered[1, 0][:, half(h)], exp_y[1][:].indirect(entries(n1_sb, h)))
         for h in range(2):
@@ -184,10 +192,10 @@ def tile_picked_nce8_none_po_kernel(
         for t, i in ((2, 0), (1, 2), (2, 1)):
             chain(t, i)
         scalar_gather(0, 0)
-        nc.scalar.activation(exp_y[3][:, :S], y_whole[3][:], ACT.Exp)
+        nc.scalar.activation(exp_y[3][:, half(1)], y_half[3, 1][:], ACT.Exp)
         add_turned(0, gathered[0, 0], first=True)
         add_turned(3, exp_y[3], first=True)
-        nc.scalar.copy(y_sb[3][:, :S], y_whole[3][:])
+        nc.scalar.copy(y_sb[3][:, half(1)], y_half[3, 1][:])
         nc.gpsimd.tensor_tensor(ratio[1], gathered[1, 2], exp_neg_y[1][:], ALU.mult)
         for i in (1, 2):
             nc.vector.tensor_copy(gathered[3, i], exp_y[3][:].indirect(lists[i][:]))
@@ -202,14 +210,13 @@ def tile_picked_nce8_none_po_kernel(
         scalar_gather(3, 0)
         for i in range(3):
             add_turned(3, gathered[3, i], last=i == 2)
-        for h in range(2):
-            exp_neg(2, h)
+        exp_neg(2, slice(0, S), y_2[:])
         for h in range(2):
             nc.gpsimd.tensor_tensor(ratio[2][:, half(h)], gathered[2, 2][:, half(h)], exp_neg_y[2][:, half(h)], ALU.mult)
 
-        log_and_turn_back(0, ("bank10", "bank11"))
+        log_and_turn_back(0, ("bank00", "bank01"))
         nc.sync.dma_start(out_rows[:, 0, :], loss[:, 0, :])
-        log_and_turn_back(3, ("bank20", "bank21"))
+        log_and_turn_back(3, ("bank30", "bank31"))
         nc.scalar.activation(loss[:, 1, :], ratio[1], ACT.Ln, bias=1.0)
         nc.sync.dma_start(out_rows[:, 1, :], loss[:, 1, :])
         for h in range(2):

@@ -199,9 +199,7 @@ def tile_picked_nce8_none_po_kernel(
         nc.gpsimd.tensor_tensor(ratio[1], gathered[1, 2], exp_neg_y[1][:], ALU.mult)
         for i in (1, 2):
             nc.vector.tensor_copy(gathered[3, i], exp_y[3][:].indirect(lists[i][:]))
-        for h in range(2):
-            looked_up = exp_y[2][:].indirect(entries(n3_sb, h))
-            nc.vector.tensor_tensor(gathered[2, 2][:, half(h)], looked_up, gathered[2, 1][:, half(h)], ALU.add)
+        chain(2, 2)
         for i in (1, 2):
             scalar_gather(0, i)
             add_turned(0, gathered[0, i])

from contextlib import ExitStack

import concourse.mybir as mybir
from concourse.masks import make_identity

K, T, S, N = 512, 2048, 512, 512
FLOPS = 2 * K * N * S

F32 = mybir.dt.float32
BF16 = mybir.dt.bfloat16
I32 = mybir.dt.int32
U32 = mybir.dt.uint32
U16 = mybir.dt.uint16
U8 = mybir.dt.uint8
FP8X4 = mybir.dt.float8_e4m3fn_x4
ACT = mybir.ActivationFunctionType
ALU = mybir.AluOpType

P = 128
PACK = 4
QUADRANTS = 4
HALF = S // 2
LIST_COLS = HALF // 16
BLOCKS = S // P
M_SCALAR = 48
J_SCALAR = 96


def half(h):
    return slice(h * HALF, (h + 1) * HALF)


def block(b):
    return slice(b * P, (b + 1) * P)


def entries(lists, h):
    return lists[:, h * LIST_COLS : (h + 1) * LIST_COLS]


def scale_rows(q):
    return slice(32 * q, 32 * q + 4), slice(4 * q, 4 * q + 4)


def tile_picked_nce8_none_po_kernel(
    tc, x_words, x_scales, w1, offs, n1, n2, n3, out_0, out_1, out_2
):
    nc = tc.nc
    with ExitStack() as ctx:
        sb = ctx.enter_context(tc.tile_pool(name="sb", bufs=1))
        ps = ctx.enter_context(tc.psum_pool(name="ps", bufs=1))

        offs_sb = sb.tile([P, S // 16], U16, name="offs_sb")
        n1_sb = sb.tile([P, S // 16], U16, name="n1_sb")
        n2_sb = sb.tile([P, S // 16], U16, name="n2_sb")
        n3_sb = sb.tile([P, S // 16], U16, name="n3_sb")
        w_raw = sb.tile([P, PACK, N], F32, name="w_raw")
        w_rows = w1.rearrange("(p j) c -> p j c", j=PACK)
        x_table = sb.tile([P, T], U32, name="x_table")
        xs_table = sb.tile([P, T], U8, name="xs_table")

        nc.vector.memset(xs_table[:, : T // 2].bitcast(I32), 0)
        nc.gpsimd.memset(xs_table[:, T // 2 :].bitcast(I32), 0)
        nc.sync.dma_start(w_raw[:, :2, :], w_rows[:, :2, :])
        nc.sync.dma_start(offs_sb[:], offs)
        for r in range(4):
            nc.sync.dma_start(xs_table[r:P:32, :].bitcast(I32), x_scales[0, r:16:4, :].bitcast(I32))
        nc.sync.dma_start(w_raw[:, 2:, :], w_rows[:, 2:, :])
        nc.sync.dma_start(x_table[:].bitcast(I32), x_words[0].rearrange("p n j -> p (n j)").bitcast(I32))
        nc.sync.dma_start(n1_sb[:], n1)
        nc.sync.dma_start(n2_sb[:], n2)
        nc.sync.dma_start(n3_sb[:], n3)

        w_bf = sb.tile([P, PACK * N], BF16, name="w_bf", tag="staging", align_bytes=64)
        w_dealt = w_bf[:].rearrange("p (t m j) -> p m t j", t=PACK, j=PACK)
        x_picked_scales = sb.tile([P, S], U8, name="x_picked_scales", align_bytes=64)
        nc.vector.tensor_copy(x_picked_scales[:], xs_table[:].indirect(offs_sb[:]))
        w_cols = w_raw[:].rearrange("p j (m t) -> p m t j", t=PACK)
        for pair in (slice(0, 2), slice(2, 4)):
            nc.scalar.copy(w_dealt[:, :M_SCALAR, :, pair], w_cols[:, :M_SCALAR, :, pair])
        nc.vector.tensor_copy(w_dealt[:, M_SCALAR:], w_cols[:, M_SCALAR:])
        w_codes = sb.tile([P, N], U32, name="w_codes", align_bytes=64)
        w_scales = sb.tile([P, N], U8, name="w_scales", align_bytes=64)
        nc.vector.quantize_mx(out=w_codes[:].bitcast(FP8X4), scales=w_scales[:], in_=w_bf[:])

        x_picked = sb.tile([P, S], U32, name="x_picked", tag="staging", align_bytes=64)
        for cols in (block(0), block(1), half(1)):
            nc.vector.tensor_copy(x_picked[:, cols], x_table[:].indirect(offs_sb[:, cols.start // 16 : cols.stop // 16]))

        identity = sb.tile([P, P], F32, name="identity")
        make_identity(nc, identity[:])

        def product(out, t, cols):
            nc.tensor.matmul_mx(
                out=out,
                lhsT=w_codes[:, block(t)].bitcast(FP8X4),
                lhsT_scale=w_scales[:, block(t)],
                rhs=x_picked[:, cols].bitcast(FP8X4),
                rhs_scale=x_picked_scales[:, cols],
                start=True,
                stop=True,
            )

        y_1 = [ps.tile([P, P], F32, name="y_1%d" % b, tag="bank_a%d" % b) for b in range(2)]
        y_half = {}
        for t, h in ((0, 0), (3, 0), (1, 1), (0, 1), (3, 1)):
            y_half[t, h] = ps.tile([P, HALF], F32, name="y_half%d%d" % (t, h), tag="bank%d%d" % (t, h))
        y_2 = ps.tile([P, S], F32, name="y_2")
        for b in range(2):
            product(y_1[b][:], 1, block(b))
            product(y_half[0, 0][:, block(b)], 0, block(b))
        for t, h in ((3, 0), (1, 1), (0, 1)):
            product(y_half[t, h][:], t, half(h))
        product(y_2[:], 2, slice(0, S))
        product(y_half[3, 1][:], 3, half(1))

        lists = (n1_sb, n2_sb, n3_sb)
        exp_y = [sb.tile([P, width], F32, name="exp_y%d" % t) for t, width in enumerate((S, 2 * S, 2 * S, 2 * S))]
        y_sb = {t: sb.tile([P, 2 * S], F32, name="y_sb%d" % t) for t in (0, 3)}
        exp_neg_y = {t: sb.tile([P, S], F32, name="exp_neg_y%d" % t) for t in (1, 2)}
        loss = sb.tile([P, PACK, S], F32, name="loss")
        ratio_2 = sb.tile([P, S], F32, name="ratio_2")
        ratio = {1: loss[:, 2, :], 2: ratio_2[:]}
        last_link = sb.tile([P, S], F32, name="last_link")
        gathered = {(1, 2): last_link[:], (2, 2): last_link[:], (3, 2): loss[:, 1, :]}
        for t in range(PACK):
            for i in range(len(lists)):
                if (t, i) not in gathered:
                    own_bytes = sb.tile([P, S], F32, name="gathered%d%d" % (t, i))
                    gathered[t, i] = own_bytes[:]
        turned_sum = {}
        turned_log = {t: sb.tile([P, S], F32, name="turned_log%d" % t) for t in (0, 3)}
        loss_bf = [sb.tile([P, HALF * PACK], BF16, name="loss_bf%d" % h, align_bytes=64) for h in range(2)]
        out_codes = sb.tile([P, S], U32, name="out_codes", align_bytes=64)
        out_scales = sb.tile([P, S], U8, name="out_scales", align_bytes=64)
        out_rows = out_0.rearrange("(p t) j -> p t j", t=PACK)
        out_words = out_1[0].rearrange("p n j -> p (n j)").bitcast(I32)

        def scalar_gather(t, i):
            nc.scalar.activation(gathered[t, i], y_sb[t][:].indirect(lists[i][:]), ACT.Exp)

        def exp_neg(t, cols, y):
            nc.scalar.activation(exp_neg_y[t][:, cols], y, ACT.Exp, scale=-1.0)

        def chain(t, i):
            looked_up = exp_y[t][:].indirect(lists[i][:])
            if i == 0:
                nc.vector.tensor_copy(gathered[t, i], looked_up)
            else:
                nc.vector.tensor_tensor(gathered[t, i], looked_up, gathered[t, i - 1], ALU.add)

        def add_turned(t, term, first=False, last=False):
            if first:
                turned_sum[t] = ps.tile([P, S], F32, name="turned_sum%d" % t, tag="bank_a%d" % (t // 3))
            for b in range(BLOCKS):
                nc.tensor.matmul(
                    turned_sum[t][:, block(b)],
                    term[:, block(b)],
                    identity[:],
                    is_transpose=True,
                    start=first and b == 0,
                    stop=last and b == BLOCKS - 1,
                )

        def log_and_turn_back(t, free_banks):
            for h in range(2):
                nc.scalar.activation(turned_log[t][:, half(h)], turned_sum[t][:, half(h)], ACT.Ln)
                log_sum = ps.tile([P, HALF], F32, name="log_sum%d%d" % (t, h), tag=free_banks[h])
                for b in range(BLOCKS // 2):
                    nc.tensor.transpose(log_sum[:, block(b)], turned_log[t][:, block(2 * h + b)], identity[:])
                nc.vector.tensor_tensor(loss[:, t, half(h)], log_sum[:], y_sb[t][:, half(h)], ALU.subtract)

        def interleaved(h):
            dst = loss_bf[h][:].rearrange("p (c i t) -> p c t i", i=4, t=PACK)
            return dst, loss[:, :, half(h)].rearrange("p t (c i) -> p c t i", i=4)

        for b in range(2):
            nc.scalar.activation(exp_y[1][:, block(b)], y_1[b][:], ACT.Exp)
            exp_neg(1, block(b), y_1[b][:])
        nc.vector.tensor_copy(y_sb[0][:, half(0)], y_half[0, 0][:])
        nc.scalar.activation(exp_y[3][:, half(0)], y_half[3, 0][:], ACT.Exp)
        nc.vector.tensor_copy(y_sb[3][:, half(0)], y_half[3, 0][:])
        nc.scalar.activation(exp_y[1][:, half(1)], y_half[1, 1][:], ACT.Exp)
        exp_neg(1, half(1), y_half[1, 1][:])
        nc.scalar.copy(y_sb[0][:, half(1)], y_half[0, 1][:])
        nc.scalar.activation(exp_y[2][:, :S], y_2[:], ACT.Exp)
        for h in range(2):
            nc.vector.tensor_copy(gathered[1, 0][:, half(h)], exp_y[1][:].indirect(entries(n1_sb, h)))
        for h in range(2):
            looked_up = exp_y[1][:].indirect(entries(n2_sb, h))
            nc.vector.tensor_tensor(gathered[1, 1][:, half(h)], looked_up, gathered[1, 0][:, half(h)], ALU.add)
        for t, i in ((2, 0), (1, 2), (2, 1)):
            chain(t, i)
        scalar_gather(0, 0)
        nc.scalar.activation(exp_y[3][:, half(1)], y_half[3, 1][:], ACT.Exp)
        add_turned(0, gathered[0, 0], first=True)
        add_turned(3, exp_y[3], first=True)
        nc.scalar.copy(y_sb[3][:, half(1)], y_half[3, 1][:])
        nc.gpsimd.tensor_tensor(ratio[1], gathered[1, 2], exp_neg_y[1][:], ALU.mult)
        for i in (1, 2):
            nc.vector.tensor_copy(gathered[3, i], exp_y[3][:].indirect(lists[i][:]))
        chain(2, 2)
        for i in (1, 2):
            scalar_gather(0, i)
            add_turned(0, gathered[0, i])
        nc.scalar.activation(exp_y[0][:], y_sb[0][:, :S], ACT.Exp)
        add_turned(0, exp_y[0], last=True)
        scalar_gather(3, 0)
        for i in range(3):
            add_turned(3, gathered[3, i], last=i == 2)
        exp_neg(2, slice(0, S), y_2[:])
        for h in range(2):
            nc.gpsimd.tensor_tensor(ratio[2][:, half(h)], gathered[2, 2][:, half(h)], exp_neg_y[2][:, half(h)], ALU.mult)

        log_and_turn_back(0, ("bank00", "bank01"))
        nc.sync.dma_start(out_rows[:, 0, :], loss[:, 0, :])
        log_and_turn_back(3, ("bank30", "bank31"))
        nc.scalar.activation(loss[:, 1, :], ratio[1], ACT.Ln, bias=1.0)
        nc.sync.dma_start(out_rows[:, 1, :], loss[:, 1, :])
        for h in range(2):
            nc.scalar.activation(loss[:, 2, half(h)], ratio[2][:, half(h)], ACT.Ln, bias=1.0)
        nc.sync.dma_start(out_rows[:, 2:, :], loss[:, 2:, :])

        dst, src = interleaved(0)
        nc.vector.tensor_copy(dst, src)
        dst, src = interleaved(1)
        nc.scalar.copy(dst[:, : J_SCALAR // 4], src[:, : J_SCALAR // 4])
        nc.vector.tensor_copy(dst[:, J_SCALAR // 4 :], src[:, J_SCALAR // 4 :])
        for h in range(2):
            nc.vector.quantize_mx(
                out=out_codes[:, half(h)].bitcast(FP8X4), scales=out_scales[:, half(h)], in_=loss_bf[h][:]
            )
            nc.sync.dma_start(out_words[:, half(h)], out_codes[:, half(h)].bitcast(I32))
        for q in range(QUADRANTS):
            partitions, rows = scale_rows(q)
            queue = nc.scalar if q % 2 else nc.sync
            queue.dma_start(out_2[0, rows, :].bitcast(I32), out_scales[partitions, :].bitcast(I32))
